import numpy as np
import ml_dtypes


def mxq(x, axis, fmt="e4m3"):
    dtype, down = {"e4m3": (ml_dtypes.float8_e4m3fn, 7), "e5m2": (ml_dtypes.float8_e5m2, 14)}[fmt]
    v = np.moveaxis(np.asarray(x, np.float32).astype(ml_dtypes.bfloat16).astype(np.float64), axis, -1)
    blocks = v.reshape(v.shape[:-1] + (-1, 32))
    amax = np.abs(blocks).max(-1, keepdims=True)
    byte = np.maximum(np.where(amax > 0, np.frexp(amax)[1] - 1 + 127, 0) - down, 1)
    scale = np.exp2(byte - 127.0)
    codes = (blocks / scale).astype(np.float32).astype(dtype).astype(np.float64)
    return np.moveaxis((codes * scale).reshape(v.shape), -1, axis)


WIDE = False


def mx_kscale(k):
    if not WIDE:
        return np.ones(k)
    levels = np.array([10, -10, 5, -5, 0])
    if k % 512:
        return np.exp2(np.random.permutation(np.resize(levels, k // 32))).repeat(32)
    a = np.empty((k // 512, 16))
    for p in range(k // 512):
        a[p, :8] = np.random.permutation(np.resize(levels, 8))
        for g in range(8):
            far = levels[np.abs(levels - a[p, g]) >= 10]
            a[p, g + 8] = far[np.random.randint(len(far))]
    return np.exp2(a.ravel()).repeat(32)


def f64(x):
    return np.asarray(x).astype(np.float64)


def striped(idx):
    return np.tile(idx.reshape(-1, 16).T, (8, 1)).astype(np.uint16)


def unstriped(offs):
    return offs[:16].T.reshape(-1).astype(np.int64)


def pack_weight(w):
    k, n = w.shape
    w = f64(np.asarray(w, np.float32).astype(ml_dtypes.bfloat16)).reshape(k // 32, 32, n)
    amax = np.abs(w).max(1)
    byte = np.clip(np.where(amax > 0, np.frexp(amax)[1] - 1 + 127 - 7, 1), 1, 254)
    scaled = (w * np.exp2(127.0 - byte)[:, None, :]).reshape(k, n).astype(np.float32)
    words = np.ascontiguousarray(scaled.reshape(k // 512, 128, 4, n).transpose(0, 1, 3, 2)).astype(ml_dtypes.float8_e4m3fn).view(np.uint8)
    return words, np.ascontiguousarray(byte.astype(np.uint8).reshape(k // 512, 16, n))


def unpack_weight(words, scales):
    g, p, n, _ = words.shape
    vals = np.ascontiguousarray(words).view(ml_dtypes.float8_e4m3fn).astype(np.float64) * np.repeat(np.exp2(scales.astype(np.float64) - 127.0), 8, axis=1)[..., None]
    return vals.transpose(0, 1, 3, 2).reshape(g * 512, n)


K, T, S, H, N = 1024, 2048, 512, 512, 256


def setup_inputs():
    n = np.random.standard_normal
    s = mx_kscale(K)[:, None]
    u = mx_kscale(H)
    packed_xT = pack_weight(n((K, T)) * s)
    return {
        "x_words": packed_xT[0],
        "x_scales": packed_xT[1],
        "w1": (n((K, H)) / np.sqrt(K) / s).astype(np.float32),
        "dual": (n((H, S))).astype(np.float32),
        "low": (-np.random.uniform(0.2, 1.0, (H, S))).astype(np.float32),
        "high": (np.random.uniform(0.2, 1.0, (H, S))).astype(np.float32),
        "rho": (np.random.uniform(0.5, 1.5, (H, 1)) * u[:, None]).astype(np.float32),
        "w2": (n((H, N)) / np.sqrt(H) / u[:, None]).astype(np.float32),
        "lin": (n((N, S))).astype(np.float32),
        "offs": striped(np.random.permutation(T)[:S]),
    }


def reference(x_words, x_scales, w1, dual, low, high, rho, w2, lin, offs):
    xq = unpack_weight(x_words, x_scales)[:, unstriped(offs)]
    y = mxq(f64(w1), 0, "e4m3").T @ xq
    t0 = y + 0.5 * f64(dual)
    clip = np.minimum(np.maximum(t0, f64(low)), f64(high))
    dn = 2.0 * (t0 - clip)
    rr = f64(rho) * (clip - dn + 0.3 * y)
    return (mxq(f64(w2), 0, "e4m3").T @ mxq(rr, 0, "e4m3")) + f64(lin)

@@ -1,0 +1,211 @@
+from contextlib import ExitStack
+
+import concourse.mybir as mybir
+
+K, T, S, H, N = 1024, 2048, 512, 512, 256
+FLOPS = 2 * K * H * S + 2 * H * N * S
+
+F32 = mybir.dt.float32
+BF16 = mybir.dt.bfloat16
+I32 = mybir.dt.int32
+U32 = mybir.dt.uint32
+U16 = mybir.dt.uint16
+U8 = mybir.dt.uint8
+FP8X4 = mybir.dt.float8_e4m3fn_x4
+ALU = mybir.AluOpType
+COPY = mybir.ActivationFunctionType.Copy
+
+P = 128
+PACK = 4
+PASSES = K // (P * PACK)
+HALF = S // 2
+CHUNK = 128
+CHUNKS = S // CHUNK
+
+
+def tile_picked_yosqp_relax_p_kernel(tc, x_words, x_scales, w1, dual, low, high, rho, w2, lin, offs, out):
+    nc = tc.nc
+    with ExitStack() as ctx:
+        sb = ctx.enter_context(tc.tile_pool(name="sb", bufs=1))
+        ps = ctx.enter_context(tc.psum_pool(name="ps", bufs=1))
+
+        w1_raw = [sb.tile([P, PACK, H], F32, name="w1_raw%d" % g) for g in range(PASSES)]
+        table = [sb.tile([P, T], U32, name="table%d" % g) for g in range(PASSES)]
+        table_scales = sb.tile([P, T], U8, name="table_scales")
+        offsets = sb.tile([P, S // 16], U16, name="offsets")
+        rho_sb = sb.tile([P, PACK], F32, name="rho_sb")
+        dual_sb = [sb.tile([P, 2, S], F32, name="dual%d" % u) for u in range(2)]
+        low_sb = sb.tile([P, PACK, S], F32, name="low_sb")
+        high_sb = [sb.tile([P, PACK, HALF], F32, name="high%d" % u) for u in range(2)]
+        w2_raw = sb.tile([P, PACK, N], F32, name="w2_raw")
+        lin_sb = sb.tile([P, 2, S], F32, name="lin_sb")
+
+        nc.vector.memset(table_scales[:].bitcast(I32), 0)
+        nc.scalar.dma_start(out=rho_sb[:], in_=rho.rearrange("(p t) o -> p (t o)", t=PACK))
+        nc.sync.dma_start(out=w1_raw[0][:], in_=w1[0:512, :].rearrange("(p j) c -> p j c", j=PACK))
+        nc.sync.dma_start(offsets[:], offs)
+        for q in range(4):
+            nc.scalar.dma_start(
+                out=table_scales[32 * q : 32 * q + 8, :].bitcast(I32),
+                in_=x_scales[:, 4 * q : 4 * q + 4, :].bitcast(I32),
+            )
+        nc.sync.dma_start(out=table[0][:].bitcast(I32), in_=x_words[0].rearrange("p n t -> p (n t)").bitcast(I32))
+        nc.sync.dma_start(out=w1_raw[1][:], in_=w1[512:1024, :].rearrange("(p j) c -> p j c", j=PACK))
+        nc.sync.dma_start(out=table[1][:].bitcast(I32), in_=x_words[1].rearrange("p n t -> p (n t)").bitcast(I32))
+        dual_v = dual.rearrange("(p t) j -> p t j", t=PACK)
+        high_v = high.rearrange("(p t) j -> p t j", t=PACK)
+        for u in range(2):
+            nc.sync.dma_start(out=dual_sb[u][:], in_=dual_v[:, 2 * u : 2 * u + 2, :])
+        nc.sync.dma_start(out=low_sb[:], in_=low.rearrange("(p t) j -> p t j", t=PACK))
+        nc.sync.dma_start(out=high_sb[0][:], in_=high_v[:, :, 0:HALF])
+        nc.sync.dma_start(out=w2_raw[:], in_=w2.rearrange("(p j) c -> p j c", j=PACK))
+        nc.sync.dma_start(out=high_sb[1][:], in_=high_v[:, :, HALF:S])
+        nc.sync.dma_start(out=lin_sb[:], in_=lin.rearrange("(h p) j -> p h j", p=P))
+
+        rho_clip = sb.tile([P, PACK], F32, name="rho_clip")
+        rho_y = sb.tile([P, PACK], F32, name="rho_y")
+        nc.scalar.activation(rho_clip[:], rho_sb[:], COPY, scale=3.0)
+        nc.scalar.activation(rho_y[:], rho_sb[:], COPY, scale=1.7)
+
+        w1_codes, w1_scales = [], []
+        for g in range(PASSES):
+            grouped = sb.tile([P, PACK, P, PACK], BF16, name="w1_grouped%d" % g, align_bytes=64)
+            dst = grouped[:].rearrange("p t m j -> p m j t")
+            src = w1_raw[g][:].rearrange("p j (m t) -> p m j t", t=PACK)
+            if g == 0:
+                nc.scalar.copy(dst, src)
+            else:
+                nc.scalar.copy(dst[:, 0:64], src[:, 0:64])
+                nc.vector.tensor_copy(dst[:, 64:128], src[:, 64:128])
+            codes = sb.tile([P, H], U32, name="w1_codes%d" % g, align_bytes=64)
+            scales = sb.tile([P, H], U8, name="w1_scales%d" % g, align_bytes=64)
+            nc.vector.quantize_mx(
+                out=codes[:].bitcast(FP8X4), scales=scales[:], in_=grouped[:].rearrange("p t m j -> p (t m j)")
+            )
+            w1_codes.append(codes)
+            w1_scales.append(scales)
+
+        x_sc = sb.tile([P, S], U8, name="x_sc", align_bytes=64)
+        nc.vector.tensor_copy(x_sc[:], table_scales[:].indirect(offsets[:]))
+        x0 = sb.tile([P, S], U32, name="x0", align_bytes=64)
+        nc.vector.tensor_copy(x0[:], table[0][:].indirect(offsets[:]))
+        x1 = []
+        for u in range(2):
+            xh = sb.tile([P, HALF], U32, name="x1_%d" % u, align_bytes=64)
+            nc.vector.tensor_copy(xh[:], table[1][:].indirect(offsets[:, 16 * u : 16 * u + 16]))
+            x1.append(xh)
+
+        y = {}
+        for u in range(2):
+            for t in range(PACK):
+                y[u, t] = ps.tile([P, HALF], F32, name="y%d%d" % (u, t), tag="bank%d" % (4 * u + t))
+                nc.tensor.matmul_mx(
+                    out=y[u, t][:],
+                    lhsT=w1_codes[0][:, t * P : (t + 1) * P].bitcast(FP8X4),
+                    lhsT_scale=w1_scales[0][:, t * P : (t + 1) * P],
+                    rhs=x0[:, u * HALF : (u + 1) * HALF].bitcast(FP8X4),
+                    rhs_scale=x_sc[:, u * HALF : (u + 1) * HALF],
+                    start=True,
+                    stop=False,
+                )
+        for u in range(2):
+            for t in range(PACK):
+                nc.tensor.matmul_mx(
+                    out=y[u, t][:],
+                    lhsT=w1_codes[1][:, t * P : (t + 1) * P].bitcast(FP8X4),
+                    lhsT_scale=w1_scales[1][:, t * P : (t + 1) * P],
+                    rhs=x1[u][:].bitcast(FP8X4),
+                    rhs_scale=x_sc[4:P, u * HALF : (u + 1) * HALF],
+                    start=False,
+                    stop=True,
+                )
+
+        rho_dual = sb.tile([P, PACK, S], F32, name="rho_dual")
+        for t in range(PACK):
+            nc.scalar.activation(rho_dual[:, t, :], dual_sb[t // 2][:, t % 2, :], COPY, scale=rho_sb[:, t : t + 1])
+
+        t0 = [sb.tile([P, PACK, HALF], F32, name="t0_%d" % u) for u in range(2)]
+        rest = [sb.tile([P, PACK, HALF], F32, name="rest%d" % u) for u in range(2)]
+        for tp in range(2):
+            for u in range(2):
+                for t in (2 * tp, 2 * tp + 1):
+                    cols = slice(u * HALF, (u + 1) * HALF)
+                    nc.vector.scalar_tensor_tensor(
+                        t0[u][:, t, :], dual_sb[tp][:, t % 2, cols], 0.5, y[u, t][:], ALU.mult, ALU.add
+                    )
+        for u in range(2):
+            for t in range(PACK):
+                cols = slice(u * HALF, (u + 1) * HALF)
+                nc.vector.scalar_tensor_tensor(
+                    rest[u][:, t, :], y[u, t][:], rho_y[:, t : t + 1], rho_dual[:, t, cols], ALU.mult, ALU.add
+                )
+        for u in range(2):
+            nc.vector.tensor_tensor(t0[u][:], t0[u][:], low_sb[:, :, u * HALF : (u + 1) * HALF], ALU.max)
+
+        w2_grouped = sb.tile([P, N, PACK], BF16, name="w2_grouped", align_bytes=64)
+        nc.scalar.copy(
+            w2_grouped[:].rearrange("p (c i) j -> p c j i", i=2),
+            w2_raw[:].rearrange("p j (c i) -> p c j i", i=2),
+        )
+        w2_codes = sb.tile([P, N], U32, name="w2_codes", align_bytes=64)
+        w2_scales = sb.tile([P, N], U8, name="w2_scales", align_bytes=64)
+
+        out_v = out.rearrange("(h p) j -> p h j", p=P)
+        scaled, rr_bf, acc = {}, {}, {}
+
+        def clip(q):
+            u, cols = q // 2, slice((q % 2) * CHUNK, (q % 2 + 1) * CHUNK)
+            c = sb.tile([P, PACK, CHUNK], F32, name="clip%d" % q)
+            nc.vector.tensor_tensor(c[:], t0[u][:, :, cols], high_sb[u][:, :, cols], ALU.min)
+            scaled[q] = sb.tile([P, PACK, CHUNK], F32, name="scaled%d" % q)
+            for t in range(PACK):
+                nc.scalar.activation(scaled[q][:, t, :], c[:, t, :], COPY, scale=rho_clip[:, t : t + 1])
+
+        def residual(q):
+            u, cols = q // 2, slice((q % 2) * CHUNK, (q % 2 + 1) * CHUNK)
+            rr_bf[q] = sb.tile([P, CHUNK, PACK], BF16, name="rr%d" % q, align_bytes=64)
+            nc.vector.tensor_tensor(
+                rr_bf[q][:].rearrange("p (c i) t -> p c t i", i=2),
+                scaled[q][:].rearrange("p t (c i) -> p c t i", i=2),
+                rest[u][:, :, cols].rearrange("p t (c i) -> p c t i", i=2),
+                ALU.subtract,
+            )
+
+        def product(q):
+            codes = sb.tile([P, CHUNK], U32, name="rr_codes%d" % q, align_bytes=64)
+            scales = sb.tile([P, CHUNK], U8, name="rr_scales%d" % q, align_bytes=64)
+            nc.vector.quantize_mx(
+                out=codes[:].bitcast(FP8X4), scales=scales[:], in_=rr_bf[q][:].rearrange("p j t -> p (j t)")
+            )
+            acc[q] = ps.tile([P, 2, CHUNK], F32, name="acc%d" % q, tag="bank%d" % q)
+            for h in range(2):
+                nc.tensor.matmul_mx(
+                    out=acc[q][:, h, :],
+                    lhsT=w2_codes[:, h * P : (h + 1) * P].bitcast(FP8X4),
+                    lhsT_scale=w2_scales[:, h * P : (h + 1) * P],
+                    rhs=codes[:].bitcast(FP8X4),
+                    rhs_scale=scales[:],
+                    start=True,
+                    stop=True,
+                )
+
+        def finish(q):
+            cols = slice(q * CHUNK, (q + 1) * CHUNK)
+            res = sb.tile([P, 2, CHUNK], F32, name="res%d" % q)
+            nc.vector.tensor_tensor(res[:], acc[q][:], lin_sb[:, :, cols], ALU.add)
+            nc.sync.dma_start(out=out_v[:, :, cols], in_=res[:])
+
+        clip(0)
+        clip(1)
+        nc.vector.quantize_mx(
+            out=w2_codes[:].bitcast(FP8X4), scales=w2_scales[:], in_=w2_grouped[:].rearrange("p c j -> p (c j)")
+        )
+        for step in range(CHUNKS + 2):
+            if step < CHUNKS:
+                residual(step)
+            if step + 2 < CHUNKS:
+                clip(step + 2)
+            if 0 <= step - 2 < CHUNKS:
+                finish(step - 2)
+            if 0 <= step - 1 < CHUNKS:
+                product(step - 1)

@@ -19,8 +19,9 @@ P = 128
 PACK = 4
 PASSES = K // (P * PACK)
 HALF = S // 2
-CHUNK = 128
-CHUNKS = S // CHUNK
+WIDTHS = (128, 128, 128, 64, 64)
+STARTS = tuple(sum(WIDTHS[:q]) for q in range(len(WIDTHS)))
+CHUNKS = len(WIDTHS)
 
 
 def tile_picked_yosqp_relax_p_kernel(tc, x_words, x_scales, w1, dual, low, high, rho, w2, lin, offs, out):
@@ -35,31 +36,37 @@ def tile_picked_yosqp_relax_p_kernel(tc, x_words, x_scales, w1, dual, low, high,
         offsets = sb.tile([P, S // 16], U16, name="offsets")
         rho_sb = sb.tile([P, PACK], F32, name="rho_sb")
         dual_sb = [sb.tile([P, 2, S], F32, name="dual%d" % u) for u in range(2)]
-        low_sb = sb.tile([P, PACK, S], F32, name="low_sb")
-        high_sb = [sb.tile([P, PACK, HALF], F32, name="high%d" % u) for u in range(2)]
+        low_sb = [sb.tile([P, 2, S], F32, name="low%d" % u) for u in range(2)]
+        high_sb = [sb.tile([P, 2, S], F32, name="high%d" % u) for u in range(2)]
         w2_raw = sb.tile([P, PACK, N], F32, name="w2_raw")
         lin_sb = sb.tile([P, 2, S], F32, name="lin_sb")
 
         nc.vector.memset(table_scales[:].bitcast(I32), 0)
-        nc.scalar.dma_start(out=rho_sb[:], in_=rho.rearrange("(p t) o -> p (t o)", t=PACK))
-        nc.sync.dma_start(out=w1_raw[0][:], in_=w1[0:512, :].rearrange("(p j) c -> p j c", j=PACK))
+        def load_scales(g):
+            for q in range(4):
+                nc.sync.dma_start(
+                    out=table_scales[32 * q + 4 * g : 32 * q + 4 * g + 4, :].bitcast(I32),
+                    in_=x_scales[g, 4 * q : 4 * q + 4, :].bitcast(I32),
+                )
+
         nc.sync.dma_start(offsets[:], offs)
-        for q in range(4):
-            nc.scalar.dma_start(
-                out=table_scales[32 * q : 32 * q + 8, :].bitcast(I32),
-                in_=x_scales[:, 4 * q : 4 * q + 4, :].bitcast(I32),
-            )
+        nc.sync.dma_start(out=w1_raw[0][:], in_=w1[0:512, :].rearrange("(p j) c -> p j c", j=PACK))
+        load_scales(0)
         nc.sync.dma_start(out=table[0][:].bitcast(I32), in_=x_words[0].rearrange("p n t -> p (n t)").bitcast(I32))
+        load_scales(1)
         nc.sync.dma_start(out=w1_raw[1][:], in_=w1[512:1024, :].rearrange("(p j) c -> p j c", j=PACK))
         nc.sync.dma_start(out=table[1][:].bitcast(I32), in_=x_words[1].rearrange("p n t -> p (n t)").bitcast(I32))
+        nc.sync.dma_start(out=rho_sb[:], in_=rho.rearrange("(p t) o -> p (t o)", t=PACK))
         dual_v = dual.rearrange("(p t) j -> p t j", t=PACK)
         high_v = high.rearrange("(p t) j -> p t j", t=PACK)
         for u in range(2):
             nc.sync.dma_start(out=dual_sb[u][:], in_=dual_v[:, 2 * u : 2 * u + 2, :])
-        nc.sync.dma_start(out=low_sb[:], in_=low.rearrange("(p t) j -> p t j", t=PACK))
-        nc.sync.dma_start(out=high_sb[0][:], in_=high_v[:, :, 0:HALF])
         nc.sync.dma_start(out=w2_raw[:], in_=w2.rearrange("(p j) c -> p j c", j=PACK))
-        nc.sync.dma_start(out=high_sb[1][:], in_=high_v[:, :, HALF:S])
+        low_v = low.rearrange("(p t) j -> p t j", t=PACK)
+        for u in range(2):
+            nc.sync.dma_start(out=low_sb[u][:], in_=low_v[:, 2 * u : 2 * u + 2, :])
+        for u in range(2):
+            nc.sync.dma_start(out=high_sb[u][:], in_=high_v[:, 2 * u : 2 * u + 2, :])
         nc.sync.dma_start(out=lin_sb[:], in_=lin.rearrange("(h p) j -> p h j", p=P))
 
         rho_clip = sb.tile([P, PACK], F32, name="rho_clip")
@@ -67,28 +74,27 @@ def tile_picked_yosqp_relax_p_kernel(tc, x_words, x_scales, w1, dual, low, high,
         nc.scalar.activation(rho_clip[:], rho_sb[:], COPY, scale=3.0)
         nc.scalar.activation(rho_y[:], rho_sb[:], COPY, scale=1.7)
 
-        w1_codes, w1_scales = [], []
-        for g in range(PASSES):
+        x_sc = sb.tile([P, S], U8, name="x_sc", align_bytes=64)
+        nc.vector.tensor_copy(x_sc[:], table_scales[:].indirect(offsets[:]))
+
+        def quantize_w1(g):
             grouped = sb.tile([P, PACK, P, PACK], BF16, name="w1_grouped%d" % g, align_bytes=64)
             dst = grouped[:].rearrange("p t m j -> p m j t")
             src = w1_raw[g][:].rearrange("p j (m t) -> p m j t", t=PACK)
-            if g == 0:
-                nc.scalar.copy(dst, src)
-            else:
-                nc.scalar.copy(dst[:, 0:64], src[:, 0:64])
-                nc.vector.tensor_copy(dst[:, 64:128], src[:, 64:128])
+            nc.scalar.copy(dst[:, 0:56], src[:, 0:56])
+            nc.vector.tensor_copy(dst[:, 56:128], src[:, 56:128])
             codes = sb.tile([P, H], U32, name="w1_codes%d" % g, align_bytes=64)
             scales = sb.tile([P, H], U8, name="w1_scales%d" % g, align_bytes=64)
             nc.vector.quantize_mx(
                 out=codes[:].bitcast(FP8X4), scales=scales[:], in_=grouped[:].rearrange("p t m j -> p (t m j)")
             )
-            w1_codes.append(codes)
-            w1_scales.append(scales)
+            return codes, scales
 
-        x_sc = sb.tile([P, S], U8, name="x_sc", align_bytes=64)
-        nc.vector.tensor_copy(x_sc[:], table_scales[:].indirect(offsets[:]))
+        w1_codes, w1_scales = [None, None], [None, None]
+        w1_codes[0], w1_scales[0] = quantize_w1(0)
         x0 = sb.tile([P, S], U32, name="x0", align_bytes=64)
         nc.vector.tensor_copy(x0[:], table[0][:].indirect(offsets[:]))
+        w1_codes[1], w1_scales[1] = quantize_w1(1)
         x1 = []
         for u in range(2):
             xh = sb.tile([P, HALF], U32, name="x1_%d" % u, align_bytes=64)
@@ -124,60 +130,67 @@ def tile_picked_yosqp_relax_p_kernel(tc, x_words, x_scales, w1, dual, low, high,
         for t in range(PACK):
             nc.scalar.activation(rho_dual[:, t, :], dual_sb[t // 2][:, t % 2, :], COPY, scale=rho_sb[:, t : t + 1])
 
-        t0 = [sb.tile([P, PACK, HALF], F32, name="t0_%d" % u) for u in range(2)]
-        rest = [sb.tile([P, PACK, HALF], F32, name="rest%d" % u) for u in range(2)]
+        w2_grouped = sb.tile([P, N, PACK], BF16, name="w2_grouped", align_bytes=64)
+        nc.scalar.copy(
+            w2_grouped[:].rearrange("p (c i) j -> p c j i", i=4),
+            w2_raw[:].rearrange("p j (c i) -> p c j i", i=4),
+        )
+
+        t0 = [sb.tile([P, 2, S], F32, name="t0_%d" % tp) for tp in range(2)]
+        rest = sb.tile([P, PACK, S], F32, name="rest")
         for tp in range(2):
             for u in range(2):
                 for t in (2 * tp, 2 * tp + 1):
                     cols = slice(u * HALF, (u + 1) * HALF)
                     nc.vector.scalar_tensor_tensor(
-                        t0[u][:, t, :], dual_sb[tp][:, t % 2, cols], 0.5, y[u, t][:], ALU.mult, ALU.add
+                        t0[tp][:, t % 2, cols], dual_sb[tp][:, t % 2, cols], 0.5, y[u, t][:], ALU.mult, ALU.add
                     )
-        for u in range(2):
-            for t in range(PACK):
+        for t in range(PACK):
+            for u in range(2):
                 cols = slice(u * HALF, (u + 1) * HALF)
                 nc.vector.scalar_tensor_tensor(
-                    rest[u][:, t, :], y[u, t][:], rho_y[:, t : t + 1], rho_dual[:, t, cols], ALU.mult, ALU.add
+                    rest[:, t, cols], y[u, t][:], rho_y[:, t : t + 1], rho_dual[:, t, cols], ALU.mult, ALU.add
                 )
-        for u in range(2):
-            nc.vector.tensor_tensor(t0[u][:], t0[u][:], low_sb[:, :, u * HALF : (u + 1) * HALF], ALU.max)
+        for tp in range(2):
+            nc.vector.tensor_tensor(t0[tp][:], t0[tp][:], low_sb[tp][:], ALU.max)
 
-        w2_grouped = sb.tile([P, N, PACK], BF16, name="w2_grouped", align_bytes=64)
-        nc.scalar.copy(
-            w2_grouped[:].rearrange("p (c i) j -> p c j i", i=2),
-            w2_raw[:].rearrange("p j (c i) -> p c j i", i=2),
-        )
         w2_codes = sb.tile([P, N], U32, name="w2_codes", align_bytes=64)
         w2_scales = sb.tile([P, N], U8, name="w2_scales", align_bytes=64)
+        nc.vector.quantize_mx(
+            out=w2_codes[:].bitcast(FP8X4), scales=w2_scales[:], in_=w2_grouped[:].rearrange("p c j -> p (c j)")
+        )
 
         out_v = out.rearrange("(h p) j -> p h j", p=P)
         scaled, rr_bf, acc = {}, {}, {}
 
-        def clip(q):
-            u, cols = q // 2, slice((q % 2) * CHUNK, (q % 2 + 1) * CHUNK)
-            c = sb.tile([P, PACK, CHUNK], F32, name="clip%d" % q)
-            nc.vector.tensor_tensor(c[:], t0[u][:, :, cols], high_sb[u][:, :, cols], ALU.min)
-            scaled[q] = sb.tile([P, PACK, CHUNK], F32, name="scaled%d" % q)
+        clip_a = sb.tile([P, 2, S], F32, name="clip_a")
+        nc.vector.tensor_tensor(clip_a[:], t0[0][:], high_sb[0][:], ALU.min)
+        for q in range(CHUNKS):
+            cols = slice(STARTS[q], STARTS[q] + WIDTHS[q])
+            clip_b = sb.tile([P, 2, WIDTHS[q]], F32, name="clip_b%d" % q)
+            nc.vector.tensor_tensor(clip_b[:], t0[1][:, :, cols], high_sb[1][:, :, cols], ALU.min)
+            scaled[q] = sb.tile([P, PACK, WIDTHS[q]], F32, name="scaled%d" % q)
             for t in range(PACK):
-                nc.scalar.activation(scaled[q][:, t, :], c[:, t, :], COPY, scale=rho_clip[:, t : t + 1])
+                src = clip_a[:, t, cols] if t < 2 else clip_b[:, t - 2, :]
+                nc.scalar.activation(scaled[q][:, t, :], src, COPY, scale=rho_clip[:, t : t + 1])
 
         def residual(q):
-            u, cols = q // 2, slice((q % 2) * CHUNK, (q % 2 + 1) * CHUNK)
-            rr_bf[q] = sb.tile([P, CHUNK, PACK], BF16, name="rr%d" % q, align_bytes=64)
+            cols = slice(STARTS[q], STARTS[q] + WIDTHS[q])
+            rr_bf[q] = sb.tile([P, WIDTHS[q], PACK], BF16, name="rr%d" % q, align_bytes=64)
             nc.vector.tensor_tensor(
                 rr_bf[q][:].rearrange("p (c i) t -> p c t i", i=2),
                 scaled[q][:].rearrange("p t (c i) -> p c t i", i=2),
-                rest[u][:, :, cols].rearrange("p t (c i) -> p c t i", i=2),
+                rest[:, :, cols].rearrange("p t (c i) -> p c t i", i=2),
                 ALU.subtract,
             )
 
         def product(q):
-            codes = sb.tile([P, CHUNK], U32, name="rr_codes%d" % q, align_bytes=64)
-            scales = sb.tile([P, CHUNK], U8, name="rr_scales%d" % q, align_bytes=64)
+            codes = sb.tile([P, WIDTHS[q]], U32, name="rr_codes%d" % q, align_bytes=64)
+            scales = sb.tile([P, WIDTHS[q]], U8, name="rr_scales%d" % q, align_bytes=64)
             nc.vector.quantize_mx(
                 out=codes[:].bitcast(FP8X4), scales=scales[:], in_=rr_bf[q][:].rearrange("p j t -> p (j t)")
             )
-            acc[q] = ps.tile([P, 2, CHUNK], F32, name="acc%d" % q, tag="bank%d" % q)
+            acc[q] = ps.tile([P, 2, WIDTHS[q]], F32, name="acc%d" % q, tag="bank%d" % q)
             for h in range(2):
                 nc.tensor.matmul_mx(
                     out=acc[q][:, h, :],
@@ -190,22 +203,15 @@ def tile_picked_yosqp_relax_p_kernel(tc, x_words, x_scales, w1, dual, low, high,
                 )
 
         def finish(q):
-            cols = slice(q * CHUNK, (q + 1) * CHUNK)
-            res = sb.tile([P, 2, CHUNK], F32, name="res%d" % q)
+            cols = slice(STARTS[q], STARTS[q] + WIDTHS[q])
+            res = sb.tile([P, 2, WIDTHS[q]], F32, name="res%d" % q)
             nc.vector.tensor_tensor(res[:], acc[q][:], lin_sb[:, :, cols], ALU.add)
             nc.sync.dma_start(out=out_v[:, :, cols], in_=res[:])
 
-        clip(0)
-        clip(1)
-        nc.vector.quantize_mx(
-            out=w2_codes[:].bitcast(FP8X4), scales=w2_scales[:], in_=w2_grouped[:].rearrange("p c j -> p (c j)")
-        )
         for step in range(CHUNKS + 2):
             if step < CHUNKS:
                 residual(step)
-            if step + 2 < CHUNKS:
-                clip(step + 2)
-            if 0 <= step - 2 < CHUNKS:
-                finish(step - 2)
             if 0 <= step - 1 < CHUNKS:
                 product(step - 1)
+            if 0 <= step - 2 < CHUNKS:
+                finish(step - 2)

@@ -79,10 +79,10 @@ def tile_picked_yosqp_relax_p_kernel(tc, x_words, x_scales, w1, dual, low, high,
 
         def quantize_w1(g):
             grouped = sb.tile([P, PACK, P, PACK], BF16, name="w1_grouped%d" % g, align_bytes=64)
-            dst = grouped[:].rearrange("p t m j -> p m j t")
-            src = w1_raw[g][:].rearrange("p j (m t) -> p m j t", t=PACK)
-            nc.scalar.copy(dst[:, 0:56], src[:, 0:56])
-            nc.vector.tensor_copy(dst[:, 56:128], src[:, 56:128])
+            dst = grouped[:].rearrange("p (u e) m j -> p u m j e", e=2)
+            src = w1_raw[g][:].rearrange("p j (m u e) -> p u m j e", u=2, e=2)
+            nc.scalar.copy(dst[:, :, 0:48], src[:, :, 0:48])
+            nc.vector.tensor_copy(dst[:, :, 48:128], src[:, :, 48:128])
             codes = sb.tile([P, H], U32, name="w1_codes%d" % g, align_bytes=64)
             scales = sb.tile([P, H], U8, name="w1_scales%d" % g, align_bytes=64)
             nc.vector.quantize_mx(

@@ -17,11 +17,18 @@ COPY = mybir.ActivationFunctionType.Copy
 
 P = 128
 PACK = 4
-PASSES = K // (P * PACK)
+K_PASS = P * PACK
+PASSES = K // K_PASS
+QUADRANTS = P // 32
 HALF = S // 2
+LIST_COLS = HALF // 16
+OUT_BLOCKS = N // P
+SCALAR_M = 48
 WIDTHS = (128, 128, 128, 64, 64)
 STARTS = tuple(sum(WIDTHS[:q]) for q in range(len(WIDTHS)))
 CHUNKS = len(WIDTHS)
+PRODUCT_LAG = 1
+FINISH_LAG = 3
 
 
 def tile_picked_yosqp_relax_p_kernel(tc, x_words, x_scales, w1, dual, low, high, rho, w2, lin, offs, out):
@@ -35,38 +42,47 @@ def tile_picked_yosqp_relax_p_kernel(tc, x_words, x_scales, w1, dual, low, high,
         table_scales = sb.tile([P, T], U8, name="table_scales")
         offsets = sb.tile([P, S // 16], U16, name="offsets")
         rho_sb = sb.tile([P, PACK], F32, name="rho_sb")
-        dual_sb = [sb.tile([P, 2, S], F32, name="dual%d" % u) for u in range(2)]
-        low_sb = [sb.tile([P, 2, S], F32, name="low%d" % u) for u in range(2)]
-        high_sb = [sb.tile([P, 2, S], F32, name="high%d" % u) for u in range(2)]
+        dual_sb = [sb.tile([P, 2, S], F32, name="dual%d" % pair) for pair in range(2)]
+        low_sb = [sb.tile([P, 2, S], F32, name="low%d" % pair) for pair in range(2)]
+        high_sb = [sb.tile([P, 2, S], F32, name="high%d" % pair) for pair in range(2)]
         w2_raw = sb.tile([P, PACK, N], F32, name="w2_raw")
-        lin_sb = sb.tile([P, 2, S], F32, name="lin_sb")
+        lin_sb = sb.tile([P, OUT_BLOCKS, S], F32, name="lin_sb")
 
         nc.vector.memset(table_scales[:].bitcast(I32), 0)
+
+        def load_w1(g):
+            rows = w1[g * K_PASS : (g + 1) * K_PASS, :]
+            nc.sync.dma_start(out=w1_raw[g][:], in_=rows.rearrange("(p j) c -> p j c", j=PACK))
+
         def load_scales(g):
-            for q in range(4):
+            for r in range(QUADRANTS):
                 nc.sync.dma_start(
-                    out=table_scales[32 * q + 4 * g : 32 * q + 4 * g + 4, :].bitcast(I32),
-                    in_=x_scales[g, 4 * q : 4 * q + 4, :].bitcast(I32),
+                    out=table_scales[32 * r + 4 * g : 32 * r + 4 * g + 4, :].bitcast(I32),
+                    in_=x_scales[g, 4 * r : 4 * r + 4, :].bitcast(I32),
                 )
 
+        def load_words(g):
+            nc.sync.dma_start(out=table[g][:].bitcast(I32), in_=x_words[g].rearrange("p n t -> p (n t)").bitcast(I32))
+
+        def load_pair(tiles, src, pair):
+            planes = src.rearrange("(p t) j -> p t j", t=PACK)
+            nc.sync.dma_start(out=tiles[pair][:], in_=planes[:, 2 * pair : 2 * pair + 2, :])
+
         nc.sync.dma_start(offsets[:], offs)
-        nc.sync.dma_start(out=w1_raw[0][:], in_=w1[0:512, :].rearrange("(p j) c -> p j c", j=PACK))
+        load_w1(0)
         load_scales(0)
-        nc.sync.dma_start(out=table[0][:].bitcast(I32), in_=x_words[0].rearrange("p n t -> p (n t)").bitcast(I32))
+        load_words(0)
         load_scales(1)
-        nc.sync.dma_start(out=w1_raw[1][:], in_=w1[512:1024, :].rearrange("(p j) c -> p j c", j=PACK))
-        nc.sync.dma_start(out=table[1][:].bitcast(I32), in_=x_words[1].rearrange("p n t -> p (n t)").bitcast(I32))
+        load_w1(1)
+        load_words(1)
         nc.sync.dma_start(out=rho_sb[:], in_=rho.rearrange("(p t) o -> p (t o)", t=PACK))
-        dual_v = dual.rearrange("(p t) j -> p t j", t=PACK)
-        high_v = high.rearrange("(p t) j -> p t j", t=PACK)
-        for u in range(2):
-            nc.sync.dma_start(out=dual_sb[u][:], in_=dual_v[:, 2 * u : 2 * u + 2, :])
+        load_pair(dual_sb, dual, 0)
+        load_pair(dual_sb, dual, 1)
+        load_pair(low_sb, low, 0)
+        load_pair(high_sb, high, 0)
         nc.sync.dma_start(out=w2_raw[:], in_=w2.rearrange("(p j) c -> p j c", j=PACK))
-        low_v = low.rearrange("(p t) j -> p t j", t=PACK)
-        for u in range(2):
-            nc.sync.dma_start(out=low_sb[u][:], in_=low_v[:, 2 * u : 2 * u + 2, :])
-        for u in range(2):
-            nc.sync.dma_start(out=high_sb[u][:], in_=high_v[:, 2 * u : 2 * u + 2, :])
+        load_pair(low_sb, low, 1)
+        load_pair(high_sb, high, 1)
         nc.sync.dma_start(out=lin_sb[:], in_=lin.rearrange("(h p) j -> p h j", p=P))
 
         rho_clip = sb.tile([P, PACK], F32, name="rho_clip")
@@ -79,10 +95,10 @@ def tile_picked_yosqp_relax_p_kernel(tc, x_words, x_scales, w1, dual, low, high,
 
         def quantize_w1(g):
             grouped = sb.tile([P, PACK, P, PACK], BF16, name="w1_grouped%d" % g, align_bytes=64)
-            dst = grouped[:].rearrange("p (u e) m j -> p u m j e", e=2)
-            src = w1_raw[g][:].rearrange("p j (m u e) -> p u m j e", u=2, e=2)
-            nc.scalar.copy(dst[:, :, 0:48], src[:, :, 0:48])
-            nc.vector.tensor_copy(dst[:, :, 48:128], src[:, :, 48:128])
+            dst = grouped[:].rearrange("p (a e) m j -> p a m j e", e=2)
+            src = w1_raw[g][:].rearrange("p j (m a e) -> p a m j e", a=2, e=2)
+            nc.scalar.copy(dst[:, :, 0:SCALAR_M], src[:, :, 0:SCALAR_M])
+            nc.vector.tensor_copy(dst[:, :, SCALAR_M:P], src[:, :, SCALAR_M:P])
             codes = sb.tile([P, H], U32, name="w1_codes%d" % g, align_bytes=64)
             scales = sb.tile([P, H], U8, name="w1_scales%d" % g, align_bytes=64)
             nc.vector.quantize_mx(
@@ -90,27 +106,25 @@ def tile_picked_yosqp_relax_p_kernel(tc, x_words, x_scales, w1, dual, low, high,
             )
             return codes, scales
 
-        w1_codes, w1_scales = [None, None], [None, None]
-        w1_codes[0], w1_scales[0] = quantize_w1(0)
+        w1_codes0, w1_scales0 = quantize_w1(0)
         x0 = sb.tile([P, S], U32, name="x0", align_bytes=64)
         nc.vector.tensor_copy(x0[:], table[0][:].indirect(offsets[:]))
-        w1_codes[1], w1_scales[1] = quantize_w1(1)
-        x1 = []
+        w1_codes1, w1_scales1 = quantize_w1(1)
+        x1 = [sb.tile([P, HALF], U32, name="x1_%d" % u, align_bytes=64) for u in range(2)]
         for u in range(2):
-            xh = sb.tile([P, HALF], U32, name="x1_%d" % u, align_bytes=64)
-            nc.vector.tensor_copy(xh[:], table[1][:].indirect(offsets[:, 16 * u : 16 * u + 16]))
-            x1.append(xh)
+            nc.vector.tensor_copy(x1[u][:], table[1][:].indirect(offsets[:, LIST_COLS * u : LIST_COLS * (u + 1)]))
 
+        halves = [slice(u * HALF, (u + 1) * HALF) for u in range(2)]
         y = {}
         for u in range(2):
             for t in range(PACK):
-                y[u, t] = ps.tile([P, HALF], F32, name="y%d%d" % (u, t), tag="bank%d" % (4 * u + t))
+                y[u, t] = ps.tile([P, HALF], F32, name="y%d%d" % (u, t), tag="bank%d" % (PACK * u + t))
                 nc.tensor.matmul_mx(
                     out=y[u, t][:],
-                    lhsT=w1_codes[0][:, t * P : (t + 1) * P].bitcast(FP8X4),
-                    lhsT_scale=w1_scales[0][:, t * P : (t + 1) * P],
-                    rhs=x0[:, u * HALF : (u + 1) * HALF].bitcast(FP8X4),
-                    rhs_scale=x_sc[:, u * HALF : (u + 1) * HALF],
+                    lhsT=w1_codes0[:, t * P : (t + 1) * P].bitcast(FP8X4),
+                    lhsT_scale=w1_scales0[:, t * P : (t + 1) * P],
+                    rhs=x0[:, halves[u]].bitcast(FP8X4),
+                    rhs_scale=x_sc[:, halves[u]],
                     start=True,
                     stop=False,
                 )
@@ -118,69 +132,83 @@ def tile_picked_yosqp_relax_p_kernel(tc, x_words, x_scales, w1, dual, low, high,
             for t in range(PACK):
                 nc.tensor.matmul_mx(
                     out=y[u, t][:],
-                    lhsT=w1_codes[1][:, t * P : (t + 1) * P].bitcast(FP8X4),
-                    lhsT_scale=w1_scales[1][:, t * P : (t + 1) * P],
+                    lhsT=w1_codes1[:, t * P : (t + 1) * P].bitcast(FP8X4),
+                    lhsT_scale=w1_scales1[:, t * P : (t + 1) * P],
                     rhs=x1[u][:].bitcast(FP8X4),
-                    rhs_scale=x_sc[4:P, u * HALF : (u + 1) * HALF],
+                    rhs_scale=x_sc[4:P, halves[u]],
                     start=False,
                     stop=True,
                 )
 
+        y_term = sb.tile([P, S], F32, name="y_term")
+        for u in range(2):
+            nc.scalar.activation(y_term[:, halves[u]], y[u, 0][:], COPY, scale=rho_y[:, 0:1])
         rho_dual = sb.tile([P, PACK, S], F32, name="rho_dual")
-        for t in range(PACK):
+        nc.gpsimd.tensor_scalar(rho_dual[:, 0, :], dual_sb[0][:, 0, :], rho_sb[:, 0:1], 0.0, ALU.mult, ALU.add)
+        for t in range(1, PACK):
             nc.scalar.activation(rho_dual[:, t, :], dual_sb[t // 2][:, t % 2, :], COPY, scale=rho_sb[:, t : t + 1])
+
+        t0 = [sb.tile([P, 2, S], F32, name="t0_%d" % pair) for pair in range(2)]
+        linear = sb.tile([P, PACK, S], F32, name="linear")
+        for pair in range(2):
+            for u in range(2):
+                for e in range(2):
+                    nc.vector.scalar_tensor_tensor(
+                        t0[pair][:, e, halves[u]],
+                        dual_sb[pair][:, e, halves[u]],
+                        0.5,
+                        y[u, 2 * pair + e][:],
+                        ALU.mult,
+                        ALU.add,
+                    )
+        nc.gpsimd.tensor_tensor(linear[:, 0, :], y_term[:], rho_dual[:, 0, :], ALU.add)
+        for t in range(1, PACK):
+            for u in range(2):
+                nc.vector.scalar_tensor_tensor(
+                    linear[:, t, halves[u]], y[u, t][:], rho_y[:, t : t + 1], rho_dual[:, t, halves[u]], ALU.mult, ALU.add
+                )
+
+        chunks = [slice(STARTS[q], STARTS[q] + WIDTHS[q]) for q in range(CHUNKS)]
+        scaled = [sb.tile([P, PACK, WIDTHS[q]], F32, name="scaled%d" % q) for q in range(CHUNKS)]
+
+        for e in range(2):
+            nc.vector.tensor_tensor(t0[0][:, e, :], t0[0][:, e, :], low_sb[0][:, e, :], ALU.max)
+        clip_first = sb.tile([P, 2, S], F32, name="clip_first")
+        for e in range(2):
+            nc.vector.tensor_tensor(clip_first[:, e, :], t0[0][:, e, :], high_sb[0][:, e, :], ALU.min)
 
         w2_grouped = sb.tile([P, N, PACK], BF16, name="w2_grouped", align_bytes=64)
         nc.scalar.copy(
             w2_grouped[:].rearrange("p (c i) j -> p c j i", i=4),
             w2_raw[:].rearrange("p j (c i) -> p c j i", i=4),
         )
+        for q in range(CHUNKS):
+            for e in range(2):
+                nc.scalar.activation(scaled[q][:, e, :], clip_first[:, e, chunks[q]], COPY, scale=rho_clip[:, e : e + 1])
 
-        t0 = [sb.tile([P, 2, S], F32, name="t0_%d" % tp) for tp in range(2)]
-        rest = sb.tile([P, PACK, S], F32, name="rest")
-        for tp in range(2):
-            for u in range(2):
-                for t in (2 * tp, 2 * tp + 1):
-                    cols = slice(u * HALF, (u + 1) * HALF)
-                    nc.vector.scalar_tensor_tensor(
-                        t0[tp][:, t % 2, cols], dual_sb[tp][:, t % 2, cols], 0.5, y[u, t][:], ALU.mult, ALU.add
-                    )
-        for t in range(PACK):
-            for u in range(2):
-                cols = slice(u * HALF, (u + 1) * HALF)
-                nc.vector.scalar_tensor_tensor(
-                    rest[:, t, cols], y[u, t][:], rho_y[:, t : t + 1], rho_dual[:, t, cols], ALU.mult, ALU.add
-                )
-        for tp in range(2):
-            nc.vector.tensor_tensor(t0[tp][:], t0[tp][:], low_sb[tp][:], ALU.max)
-
+        nc.vector.tensor_tensor(t0[1][:], t0[1][:], low_sb[1][:], ALU.max)
         w2_codes = sb.tile([P, N], U32, name="w2_codes", align_bytes=64)
         w2_scales = sb.tile([P, N], U8, name="w2_scales", align_bytes=64)
         nc.vector.quantize_mx(
             out=w2_codes[:].bitcast(FP8X4), scales=w2_scales[:], in_=w2_grouped[:].rearrange("p c j -> p (c j)")
         )
-
-        out_v = out.rearrange("(h p) j -> p h j", p=P)
-        scaled, rr_bf, acc = {}, {}, {}
-
-        clip_a = sb.tile([P, 2, S], F32, name="clip_a")
-        nc.vector.tensor_tensor(clip_a[:], t0[0][:], high_sb[0][:], ALU.min)
         for q in range(CHUNKS):
-            cols = slice(STARTS[q], STARTS[q] + WIDTHS[q])
-            clip_b = sb.tile([P, 2, WIDTHS[q]], F32, name="clip_b%d" % q)
-            nc.vector.tensor_tensor(clip_b[:], t0[1][:, :, cols], high_sb[1][:, :, cols], ALU.min)
-            scaled[q] = sb.tile([P, PACK, WIDTHS[q]], F32, name="scaled%d" % q)
-            for t in range(PACK):
-                src = clip_a[:, t, cols] if t < 2 else clip_b[:, t - 2, :]
-                nc.scalar.activation(scaled[q][:, t, :], src, COPY, scale=rho_clip[:, t : t + 1])
+            clip_second = sb.tile([P, 2, WIDTHS[q]], F32, name="clip_second%d" % q)
+            nc.vector.tensor_tensor(clip_second[:], t0[1][:, :, chunks[q]], high_sb[1][:, :, chunks[q]], ALU.min)
+            for e in range(2):
+                nc.scalar.activation(
+                    scaled[q][:, 2 + e, :], clip_second[:, e, :], COPY, scale=rho_clip[:, 2 + e : 3 + e]
+                )
+
+        out_blocks = out.rearrange("(h p) j -> p h j", p=P)
+        rr, acc = {}, {}
 
         def residual(q):
-            cols = slice(STARTS[q], STARTS[q] + WIDTHS[q])
-            rr_bf[q] = sb.tile([P, WIDTHS[q], PACK], BF16, name="rr%d" % q, align_bytes=64)
+            rr[q] = sb.tile([P, WIDTHS[q], PACK], BF16, name="rr%d" % q, align_bytes=64)
             nc.vector.tensor_tensor(
-                rr_bf[q][:].rearrange("p (c i) t -> p c t i", i=2),
+                rr[q][:].rearrange("p (c i) t -> p c t i", i=2),
                 scaled[q][:].rearrange("p t (c i) -> p c t i", i=2),
-                rest[:, :, cols].rearrange("p t (c i) -> p c t i", i=2),
+                linear[:, :, chunks[q]].rearrange("p t (c i) -> p c t i", i=2),
                 ALU.subtract,
             )
 
@@ -188,10 +216,10 @@ def tile_picked_yosqp_relax_p_kernel(tc, x_words, x_scales, w1, dual, low, high,
             codes = sb.tile([P, WIDTHS[q]], U32, name="rr_codes%d" % q, align_bytes=64)
             scales = sb.tile([P, WIDTHS[q]], U8, name="rr_scales%d" % q, align_bytes=64)
             nc.vector.quantize_mx(
-                out=codes[:].bitcast(FP8X4), scales=scales[:], in_=rr_bf[q][:].rearrange("p j t -> p (j t)")
+                out=codes[:].bitcast(FP8X4), scales=scales[:], in_=rr[q][:].rearrange("p j t -> p (j t)")
             )
-            acc[q] = ps.tile([P, 2, WIDTHS[q]], F32, name="acc%d" % q, tag="bank%d" % q)
-            for h in range(2):
+            acc[q] = ps.tile([P, OUT_BLOCKS, WIDTHS[q]], F32, name="acc%d" % q, tag="bank%d" % q)
+            for h in range(OUT_BLOCKS):
                 nc.tensor.matmul_mx(
                     out=acc[q][:, h, :],
                     lhsT=w2_codes[:, h * P : (h + 1) * P].bitcast(FP8X4),
@@ -203,15 +231,14 @@ def tile_picked_yosqp_relax_p_kernel(tc, x_words, x_scales, w1, dual, low, high,
                 )
 
         def finish(q):
-            cols = slice(STARTS[q], STARTS[q] + WIDTHS[q])
-            res = sb.tile([P, 2, WIDTHS[q]], F32, name="res%d" % q)
-            nc.vector.tensor_tensor(res[:], acc[q][:], lin_sb[:, :, cols], ALU.add)
-            nc.sync.dma_start(out=out_v[:, :, cols], in_=res[:])
+            res = sb.tile([P, OUT_BLOCKS, WIDTHS[q]], F32, name="res%d" % q)
+            nc.vector.tensor_tensor(res[:], acc[q][:], lin_sb[:, :, chunks[q]], ALU.add)
+            nc.sync.dma_start(out=out_blocks[:, :, chunks[q]], in_=res[:])
 
-        for step in range(CHUNKS + 2):
+        for step in range(CHUNKS + FINISH_LAG):
             if step < CHUNKS:
                 residual(step)
-            if 0 <= step - 1 < CHUNKS:
-                product(step - 1)
-            if 0 <= step - 2 < CHUNKS:
-                finish(step - 2)
+            if PRODUCT_LAG <= step < CHUNKS + PRODUCT_LAG:
+                product(step - PRODUCT_LAG)
+            if step >= FINISH_LAG:
+                finish(step - FINISH_LAG)

@@ -54,12 +54,13 @@ def tile_picked_yosqp_relax_p_kernel(tc, x_words, x_scales, w1, dual, low, high,
             rows = w1[g * K_PASS : (g + 1) * K_PASS, :]
             nc.sync.dma_start(out=w1_raw[g][:], in_=rows.rearrange("(p j) c -> p j c", j=PACK))
 
-        def load_scales(g):
-            for r in range(QUADRANTS):
-                nc.sync.dma_start(
-                    out=table_scales[32 * r + 4 * g : 32 * r + 4 * g + 4, :].bitcast(I32),
-                    in_=x_scales[g, 4 * r : 4 * r + 4, :].bitcast(I32),
-                )
+        def load_scales(rows):
+            for q in rows:
+                for g in range(PASSES):
+                    nc.sync.dma_start(
+                        out=table_scales[4 * g + q : P : 32, :].bitcast(I32),
+                        in_=x_scales[g, q : 4 * QUADRANTS : 4, :].bitcast(I32),
+                    )
 
         def load_words(g):
             nc.sync.dma_start(out=table[g][:].bitcast(I32), in_=x_words[g].rearrange("p n t -> p (n t)").bitcast(I32))
@@ -70,9 +71,9 @@ def tile_picked_yosqp_relax_p_kernel(tc, x_words, x_scales, w1, dual, low, high,
 
         nc.sync.dma_start(offsets[:], offs)
         load_w1(0)
-        load_scales(0)
+        load_scales((0, 1))
         load_words(0)
-        load_scales(1)
+        load_scales((2, 3))
         load_w1(1)
         load_words(1)
         nc.sync.dma_start(out=rho_sb[:], in_=rho.rearrange("(p t) o -> p (t o)", t=PACK))

@@ -43,7 +43,7 @@ def tile_picked_yosqp_relax_p_kernel(tc, x_words, x_scales, w1, dual, low, high,
         offsets = sb.tile([P, S // 16], U16, name="offsets")
         rho_sb = sb.tile([P, PACK], F32, name="rho_sb")
         dual_sb = [sb.tile([P, 2, S], F32, name="dual%d" % pair) for pair in range(2)]
-        low_sb = [sb.tile([P, 2, S], F32, name="low%d" % pair) for pair in range(2)]
+        low_sb = sb.tile([P, PACK, S], F32, name="low")
         high_sb = [sb.tile([P, 2, S], F32, name="high%d" % pair) for pair in range(2)]
         w2_raw = sb.tile([P, PACK, N], F32, name="w2_raw")
         lin_sb = sb.tile([P, OUT_BLOCKS, S], F32, name="lin_sb")
@@ -79,20 +79,19 @@ def tile_picked_yosqp_relax_p_kernel(tc, x_words, x_scales, w1, dual, low, high,
         nc.sync.dma_start(out=rho_sb[:], in_=rho.rearrange("(p t) o -> p (t o)", t=PACK))
         load_pair(dual_sb, dual, 0)
         load_pair(dual_sb, dual, 1)
-        load_pair(low_sb, low, 0)
+        nc.sync.dma_start(out=low_sb[:], in_=low.rearrange("(p t) j -> p t j", t=PACK))
         load_pair(high_sb, high, 0)
         nc.sync.dma_start(out=w2_raw[:], in_=w2.rearrange("(p j) c -> p j c", j=PACK))
-        load_pair(low_sb, low, 1)
         load_pair(high_sb, high, 1)
         nc.sync.dma_start(out=lin_sb[:], in_=lin.rearrange("(h p) j -> p h j", p=P))
 
         rho_clip = sb.tile([P, PACK], F32, name="rho_clip")
-        rho_y = sb.tile([P, PACK], F32, name="rho_y")
         nc.scalar.activation(rho_clip[:], rho_sb[:], COPY, scale=3.0)
-        nc.scalar.activation(rho_y[:], rho_sb[:], COPY, scale=1.7)
 
-        x_sc = sb.tile([P, S], U8, name="x_sc", align_bytes=64)
-        nc.vector.tensor_copy(x_sc[:], table_scales[:].indirect(offsets[:]))
+        def gather_half(name, dtype, window, u):
+            picked = sb.tile([P, HALF], dtype, name="%s_%d" % (name, u), align_bytes=64)
+            nc.vector.tensor_copy(picked[:], window[:].indirect(offsets[:, LIST_COLS * u : LIST_COLS * (u + 1)]))
+            return picked
 
         def quantize_w1(g):
             grouped = sb.tile([P, PACK, P, PACK], BF16, name="w1_grouped%d" % g, align_bytes=64)
@@ -108,12 +107,12 @@ def tile_picked_yosqp_relax_p_kernel(tc, x_words, x_scales, w1, dual, low, high,
             return codes, scales
 
         w1_codes0, w1_scales0 = quantize_w1(0)
-        x0 = sb.tile([P, S], U32, name="x0", align_bytes=64)
-        nc.vector.tensor_copy(x0[:], table[0][:].indirect(offsets[:]))
-        w1_codes1, w1_scales1 = quantize_w1(1)
-        x1 = [sb.tile([P, HALF], U32, name="x1_%d" % u, align_bytes=64) for u in range(2)]
+        x0, x_sc = [], []
         for u in range(2):
-            nc.vector.tensor_copy(x1[u][:], table[1][:].indirect(offsets[:, LIST_COLS * u : LIST_COLS * (u + 1)]))
+            x0.append(gather_half("x0", U32, table[0], u))
+            x_sc.append(gather_half("x_sc", U8, table_scales, u))
+        w1_codes1, w1_scales1 = quantize_w1(1)
+        x1 = [gather_half("x1", U32, table[1], u) for u in range(2)]
 
         halves = [slice(u * HALF, (u + 1) * HALF) for u in range(2)]
         y = {}
@@ -124,59 +123,59 @@ def tile_picked_yosqp_relax_p_kernel(tc, x_words, x_scales, w1, dual, low, high,
                     out=y[u, t][:],
                     lhsT=w1_codes0[:, t * P : (t + 1) * P].bitcast(FP8X4),
                     lhsT_scale=w1_scales0[:, t * P : (t + 1) * P],
-                    rhs=x0[:, halves[u]].bitcast(FP8X4),
-                    rhs_scale=x_sc[:, halves[u]],
+                    rhs=x0[u][:].bitcast(FP8X4),
+                    rhs_scale=x_sc[u][:],
                     start=True,
                     stop=False,
                 )
         for u in range(2):
-            for t in range(PACK):
+            for t in (0, 2, 1, 3):
                 nc.tensor.matmul_mx(
                     out=y[u, t][:],
                     lhsT=w1_codes1[:, t * P : (t + 1) * P].bitcast(FP8X4),
                     lhsT_scale=w1_scales1[:, t * P : (t + 1) * P],
                     rhs=x1[u][:].bitcast(FP8X4),
-                    rhs_scale=x_sc[4:P, halves[u]],
+                    rhs_scale=x_sc[u][4:P, :],
                     start=False,
                     stop=True,
                 )
 
-        y_term = sb.tile([P, S], F32, name="y_term")
-        for u in range(2):
-            nc.scalar.activation(y_term[:, halves[u]], y[u, 0][:], COPY, scale=rho_y[:, 0:1])
-        rho_dual = sb.tile([P, PACK, S], F32, name="rho_dual")
-        nc.gpsimd.tensor_scalar(rho_dual[:, 0, :], dual_sb[0][:, 0, :], rho_sb[:, 0:1], 0.0, ALU.mult, ALU.add)
-        for t in range(1, PACK):
-            nc.scalar.activation(rho_dual[:, t, :], dual_sb[t // 2][:, t % 2, :], COPY, scale=rho_sb[:, t : t + 1])
+        t0 = sb.tile([P, PACK, S], F32, name="t0")
 
-        t0 = [sb.tile([P, 2, S], F32, name="t0_%d" % pair) for pair in range(2)]
-        linear = sb.tile([P, PACK, S], F32, name="linear")
-        for pair in range(2):
-            for u in range(2):
-                for e in range(2):
-                    nc.vector.scalar_tensor_tensor(
-                        t0[pair][:, e, halves[u]],
-                        dual_sb[pair][:, e, halves[u]],
-                        0.5,
-                        y[u, 2 * pair + e][:],
-                        ALU.mult,
-                        ALU.add,
-                    )
-        nc.gpsimd.tensor_tensor(linear[:, 0, :], y_term[:], rho_dual[:, 0, :], ALU.add)
-        for t in range(1, PACK):
-            for u in range(2):
+        def make_t0(u, t):
+            nc.vector.scalar_tensor_tensor(
+                t0[:, t, halves[u]], dual_sb[t // 2][:, t % 2, halves[u]], 0.5, y[u, t][:], ALU.mult, ALU.add
+            )
+
+        total = sb.tile([P, PACK, S], F32, name="total")
+        for u in range(2):
+            y_term = sb.tile([P, 2, HALF], F32, name="y_term%d" % u)
+            for e in range(2):
+                nc.scalar.activation(y_term[:, e, :], y[u, 2 + e][:], COPY, scale=1.7)
+            nc.gpsimd.tensor_tensor(total[:, 2:PACK, halves[u]], y_term[:], dual_sb[1][:, :, halves[u]], ALU.add)
+        for u in range(2):
+            for t in range(2):
+                make_t0(u, t)
+        for u in range(2):
+            for t in range(2):
                 nc.vector.scalar_tensor_tensor(
-                    linear[:, t, halves[u]], y[u, t][:], rho_y[:, t : t + 1], rho_dual[:, t, halves[u]], ALU.mult, ALU.add
+                    total[:, t, halves[u]], y[u, t][:], 1.7, dual_sb[0][:, t, halves[u]], ALU.mult, ALU.add
                 )
+        for u in range(2):
+            for t in range(2, PACK):
+                make_t0(u, t)
+        linear = sb.tile([P, PACK, S], F32, name="linear")
+        for t in range(PACK):
+            nc.scalar.activation(linear[:, t, :], total[:, t, :], COPY, scale=rho_sb[:, t : t + 1])
 
         chunks = [slice(STARTS[q], STARTS[q] + WIDTHS[q]) for q in range(CHUNKS)]
         scaled = [sb.tile([P, PACK, WIDTHS[q]], F32, name="scaled%d" % q) for q in range(CHUNKS)]
 
-        for e in range(2):
-            nc.vector.tensor_tensor(t0[0][:, e, :], t0[0][:, e, :], low_sb[0][:, e, :], ALU.max)
+        for pair in range(2):
+            planes = slice(2 * pair, 2 * pair + 2)
+            nc.vector.tensor_tensor(t0[:, planes, :], t0[:, planes, :], low_sb[:, planes, :], ALU.max)
         clip_first = sb.tile([P, 2, S], F32, name="clip_first")
-        for e in range(2):
-            nc.vector.tensor_tensor(clip_first[:, e, :], t0[0][:, e, :], high_sb[0][:, e, :], ALU.min)
+        nc.vector.tensor_tensor(clip_first[:], t0[:, 0:2, :], high_sb[0][:], ALU.min)
 
         w2_grouped = sb.tile([P, N, PACK], BF16, name="w2_grouped", align_bytes=64)
         nc.scalar.copy(
@@ -187,7 +186,6 @@ def tile_picked_yosqp_relax_p_kernel(tc, x_words, x_scales, w1, dual, low, high,
             for e in range(2):
                 nc.scalar.activation(scaled[q][:, e, :], clip_first[:, e, chunks[q]], COPY, scale=rho_clip[:, e : e + 1])
 
-        nc.vector.tensor_tensor(t0[1][:], t0[1][:], low_sb[1][:], ALU.max)
         w2_codes = sb.tile([P, N], U32, name="w2_codes", align_bytes=64)
         w2_scales = sb.tile([P, N], U8, name="w2_scales", align_bytes=64)
         nc.vector.quantize_mx(
@@ -195,7 +193,7 @@ def tile_picked_yosqp_relax_p_kernel(tc, x_words, x_scales, w1, dual, low, high,
         )
         for q in range(CHUNKS):
             clip_second = sb.tile([P, 2, WIDTHS[q]], F32, name="clip_second%d" % q)
-            nc.vector.tensor_tensor(clip_second[:], t0[1][:, :, chunks[q]], high_sb[1][:, :, chunks[q]], ALU.min)
+            nc.vector.tensor_tensor(clip_second[:], t0[:, 2:PACK, chunks[q]], high_sb[1][:, :, chunks[q]], ALU.min)
             for e in range(2):
                 nc.scalar.activation(
                     scaled[q][:, 2 + e, :], clip_second[:, e, :], COPY, scale=rho_clip[:, 2 + e : 3 + e]

@@ -24,6 +24,7 @@ HALF = S // 2
 LIST_COLS = HALF // 16
 OUT_BLOCKS = N // P
 SCALAR_M = 48
+VECTOR_TAIL = 64
 WIDTHS = (128, 128, 128, 64, 64)
 STARTS = tuple(sum(WIDTHS[:q]) for q in range(len(WIDTHS)))
 CHUNKS = len(WIDTHS)
@@ -43,7 +44,7 @@ def tile_picked_yosqp_relax_p_kernel(tc, x_words, x_scales, w1, dual, low, high,
         offsets = sb.tile([P, S // 16], U16, name="offsets")
         rho_sb = sb.tile([P, PACK], F32, name="rho_sb")
         dual_sb = [sb.tile([P, 2, S], F32, name="dual%d" % pair) for pair in range(2)]
-        low_sb = sb.tile([P, PACK, S], F32, name="low")
+        low_sb = [sb.tile([P, 2, S], F32, name="low%d" % pair) for pair in range(2)]
         high_sb = [sb.tile([P, 2, S], F32, name="high%d" % pair) for pair in range(2)]
         w2_raw = sb.tile([P, PACK, N], F32, name="w2_raw")
         lin_sb = sb.tile([P, OUT_BLOCKS, S], F32, name="lin_sb")
@@ -69,8 +70,8 @@ def tile_picked_yosqp_relax_p_kernel(tc, x_words, x_scales, w1, dual, low, high,
             planes = src.rearrange("(p t) j -> p t j", t=PACK)
             nc.sync.dma_start(out=tiles[pair][:], in_=planes[:, 2 * pair : 2 * pair + 2, :])
 
-        nc.sync.dma_start(offsets[:], offs)
         load_w1(0)
+        nc.sync.dma_start(offsets[:], offs)
         load_scales((0, 1))
         load_words(0)
         load_scales((2, 3))
@@ -79,9 +80,10 @@ def tile_picked_yosqp_relax_p_kernel(tc, x_words, x_scales, w1, dual, low, high,
         nc.sync.dma_start(out=rho_sb[:], in_=rho.rearrange("(p t) o -> p (t o)", t=PACK))
         load_pair(dual_sb, dual, 0)
         load_pair(dual_sb, dual, 1)
-        nc.sync.dma_start(out=low_sb[:], in_=low.rearrange("(p t) j -> p t j", t=PACK))
+        load_pair(low_sb, low, 0)
         load_pair(high_sb, high, 0)
         nc.sync.dma_start(out=w2_raw[:], in_=w2.rearrange("(p j) c -> p j c", j=PACK))
+        load_pair(low_sb, low, 1)
         load_pair(high_sb, high, 1)
         nc.sync.dma_start(out=lin_sb[:], in_=lin.rearrange("(h p) j -> p h j", p=P))
 
@@ -148,11 +150,12 @@ def tile_picked_yosqp_relax_p_kernel(tc, x_words, x_scales, w1, dual, low, high,
             )
 
         total = sb.tile([P, PACK, S], F32, name="total")
-        for u in range(2):
-            y_term = sb.tile([P, 2, HALF], F32, name="y_term%d" % u)
+        for u, width in enumerate((HALF, HALF - VECTOR_TAIL)):
+            y_term = sb.tile([P, 2, width], F32, name="y_term%d" % u)
+            cols = slice(u * HALF, u * HALF + width)
             for e in range(2):
-                nc.scalar.activation(y_term[:, e, :], y[u, 2 + e][:], COPY, scale=1.7)
-            nc.gpsimd.tensor_tensor(total[:, 2:PACK, halves[u]], y_term[:], dual_sb[1][:, :, halves[u]], ALU.add)
+                nc.scalar.activation(y_term[:, e, :], y[u, 2 + e][:, 0:width], COPY, scale=1.7)
+            nc.gpsimd.tensor_tensor(total[:, 2:PACK, cols], y_term[:], dual_sb[1][:, :, cols], ALU.add)
         for u in range(2):
             for t in range(2):
                 make_t0(u, t)
@@ -164,40 +167,54 @@ def tile_picked_yosqp_relax_p_kernel(tc, x_words, x_scales, w1, dual, low, high,
         for u in range(2):
             for t in range(2, PACK):
                 make_t0(u, t)
+        for t in range(2, PACK):
+            nc.vector.scalar_tensor_tensor(
+                total[:, t, S - VECTOR_TAIL : S],
+                y[1, t][:, HALF - VECTOR_TAIL : HALF],
+                1.7,
+                dual_sb[1][:, t - 2, S - VECTOR_TAIL : S],
+                ALU.mult,
+                ALU.add,
+            )
         linear = sb.tile([P, PACK, S], F32, name="linear")
         for t in range(PACK):
             nc.scalar.activation(linear[:, t, :], total[:, t, :], COPY, scale=rho_sb[:, t : t + 1])
 
         chunks = [slice(STARTS[q], STARTS[q] + WIDTHS[q]) for q in range(CHUNKS)]
-        scaled = [sb.tile([P, PACK, WIDTHS[q]], F32, name="scaled%d" % q) for q in range(CHUNKS)]
+        scaled = sb.tile([P, PACK, S], F32, name="scaled")
+        clip = sb.tile([P, PACK, S], F32, name="clip")
+        first, rest = chunks[0], slice(STARTS[1], S)
 
-        for pair in range(2):
+        def upper(pair, cols):
             planes = slice(2 * pair, 2 * pair + 2)
-            nc.vector.tensor_tensor(t0[:, planes, :], t0[:, planes, :], low_sb[:, planes, :], ALU.max)
-        clip_first = sb.tile([P, 2, S], F32, name="clip_first")
-        nc.vector.tensor_tensor(clip_first[:], t0[:, 0:2, :], high_sb[0][:], ALU.min)
+            nc.vector.tensor_tensor(clip[:, planes, cols], t0[:, planes, cols], high_sb[pair][:, :, cols], ALU.min)
+
+        def scale_clip(t, cols):
+            nc.scalar.activation(scaled[:, t, cols], clip[:, t, cols], COPY, scale=rho_clip[:, t : t + 1])
+
+        for t in range(2):
+            nc.vector.tensor_tensor(t0[:, t, :], t0[:, t, :], low_sb[0][:, t, :], ALU.max)
+        for t in range(2):
+            nc.vector.tensor_tensor(clip[:, t, :], t0[:, t, :], high_sb[0][:, t, :], ALU.min)
+        nc.vector.tensor_tensor(t0[:, 2:PACK, :], t0[:, 2:PACK, :], low_sb[1][:], ALU.max)
 
         w2_grouped = sb.tile([P, N, PACK], BF16, name="w2_grouped", align_bytes=64)
         nc.scalar.copy(
             w2_grouped[:].rearrange("p (c i) j -> p c j i", i=4),
             w2_raw[:].rearrange("p j (c i) -> p c j i", i=4),
         )
-        for q in range(CHUNKS):
-            for e in range(2):
-                nc.scalar.activation(scaled[q][:, e, :], clip_first[:, e, chunks[q]], COPY, scale=rho_clip[:, e : e + 1])
-
         w2_codes = sb.tile([P, N], U32, name="w2_codes", align_bytes=64)
         w2_scales = sb.tile([P, N], U8, name="w2_scales", align_bytes=64)
         nc.vector.quantize_mx(
             out=w2_codes[:].bitcast(FP8X4), scales=w2_scales[:], in_=w2_grouped[:].rearrange("p c j -> p (c j)")
         )
-        for q in range(CHUNKS):
-            clip_second = sb.tile([P, 2, WIDTHS[q]], F32, name="clip_second%d" % q)
-            nc.vector.tensor_tensor(clip_second[:], t0[:, 2:PACK, chunks[q]], high_sb[1][:, :, chunks[q]], ALU.min)
-            for e in range(2):
-                nc.scalar.activation(
-                    scaled[q][:, 2 + e, :], clip_second[:, e, :], COPY, scale=rho_clip[:, 2 + e : 3 + e]
-                )
+        upper(1, first)
+        upper(1, rest)
+        scale_clip(0, slice(0, S))
+        scale_clip(1, slice(0, S))
+        for cols in (first, chunks[1], chunks[2], slice(STARTS[3], S)):
+            scale_clip(2, cols)
+            scale_clip(3, cols)
 
         out_blocks = out.rearrange("(h p) j -> p h j", p=P)
         rr, acc = {}, {}
@@ -206,7 +223,7 @@ def tile_picked_yosqp_relax_p_kernel(tc, x_words, x_scales, w1, dual, low, high,
             rr[q] = sb.tile([P, WIDTHS[q], PACK], BF16, name="rr%d" % q, align_bytes=64)
             nc.vector.tensor_tensor(
                 rr[q][:].rearrange("p (c i) t -> p c t i", i=2),
-                scaled[q][:].rearrange("p t (c i) -> p c t i", i=2),
+                scaled[:, :, chunks[q]].rearrange("p t (c i) -> p c t i", i=2),
                 linear[:, :, chunks[q]].rearrange("p t (c i) -> p c t i", i=2),
                 ALU.subtract,
             )

@@ -29,7 +29,7 @@ WIDTHS = (128, 128, 128, 64, 64)
 STARTS = tuple(sum(WIDTHS[:q]) for q in range(len(WIDTHS)))
 CHUNKS = len(WIDTHS)
 PRODUCT_LAG = 1
-FINISH_LAG = 3
+FINISH_LAG = 4
 
 
 def tile_picked_yosqp_relax_p_kernel(tc, x_words, x_scales, w1, dual, low, high, rho, w2, lin, offs, out):
@@ -43,10 +43,12 @@ def tile_picked_yosqp_relax_p_kernel(tc, x_words, x_scales, w1, dual, low, high,
         table_scales = sb.tile([P, T], U8, name="table_scales")
         offsets = sb.tile([P, S // 16], U16, name="offsets")
         rho_sb = sb.tile([P, PACK], F32, name="rho_sb")
-        dual_sb = [sb.tile([P, 2, S], F32, name="dual%d" % pair) for pair in range(2)]
+        dual_first = [sb.tile([P, S], F32, name="dual%d" % t) for t in range(2)]
+        dual_second = sb.tile([P, 2, S], F32, name="dual_second")
+        dual_plane = [dual_first[0][:], dual_first[1][:], dual_second[:, 0, :], dual_second[:, 1, :]]
         low_sb = [sb.tile([P, 2, S], F32, name="low%d" % pair) for pair in range(2)]
         high_sb = [sb.tile([P, 2, S], F32, name="high%d" % pair) for pair in range(2)]
-        w2_raw = sb.tile([P, PACK, N], F32, name="w2_raw")
+        w2_raw = sb.tile([P, PACK, N], F32, name="w2_raw", tag="w2_raw")
         lin_sb = sb.tile([P, OUT_BLOCKS, S], F32, name="lin_sb")
 
         nc.vector.memset(table_scales[:].bitcast(I32), 0)
@@ -77,9 +79,11 @@ def tile_picked_yosqp_relax_p_kernel(tc, x_words, x_scales, w1, dual, low, high,
         load_scales((2, 3))
         load_w1(1)
         load_words(1)
+        dual_planes = dual.rearrange("(p t) j -> p t j", t=PACK)
+        nc.sync.dma_start(out=dual_first[0][:], in_=dual_planes[:, 0, :])
+        nc.sync.dma_start(out=dual_second[:], in_=dual_planes[:, 2:PACK, :])
+        nc.sync.dma_start(out=dual_first[1][:], in_=dual_planes[:, 1, :])
         nc.sync.dma_start(out=rho_sb[:], in_=rho.rearrange("(p t) o -> p (t o)", t=PACK))
-        load_pair(dual_sb, dual, 0)
-        load_pair(dual_sb, dual, 1)
         load_pair(low_sb, low, 0)
         load_pair(high_sb, high, 0)
         nc.sync.dma_start(out=w2_raw[:], in_=w2.rearrange("(p j) c -> p j c", j=PACK))
@@ -131,7 +135,7 @@ def tile_picked_yosqp_relax_p_kernel(tc, x_words, x_scales, w1, dual, low, high,
                     stop=False,
                 )
         for u in range(2):
-            for t in (0, 2, 1, 3):
+            for t in (0, 2, 3, 1):
                 nc.tensor.matmul_mx(
                     out=y[u, t][:],
                     lhsT=w1_codes1[:, t * P : (t + 1) * P].bitcast(FP8X4),
@@ -146,7 +150,7 @@ def tile_picked_yosqp_relax_p_kernel(tc, x_words, x_scales, w1, dual, low, high,
 
         def make_t0(u, t):
             nc.vector.scalar_tensor_tensor(
-                t0[:, t, halves[u]], dual_sb[t // 2][:, t % 2, halves[u]], 0.5, y[u, t][:], ALU.mult, ALU.add
+                t0[:, t, halves[u]], dual_plane[t][:, halves[u]], 0.5, y[u, t][:], ALU.mult, ALU.add
             )
 
         total = sb.tile([P, PACK, S], F32, name="total")
@@ -155,14 +159,12 @@ def tile_picked_yosqp_relax_p_kernel(tc, x_words, x_scales, w1, dual, low, high,
             cols = slice(u * HALF, u * HALF + width)
             for e in range(2):
                 nc.scalar.activation(y_term[:, e, :], y[u, 2 + e][:, 0:width], COPY, scale=1.7)
-            nc.gpsimd.tensor_tensor(total[:, 2:PACK, cols], y_term[:], dual_sb[1][:, :, cols], ALU.add)
-        for u in range(2):
-            for t in range(2):
+            nc.gpsimd.tensor_tensor(total[:, 2:PACK, cols], y_term[:], dual_second[:, :, cols], ALU.add)
+        for t in range(2):
+            for u in range(2):
                 make_t0(u, t)
-        for u in range(2):
-            for t in range(2):
                 nc.vector.scalar_tensor_tensor(
-                    total[:, t, halves[u]], y[u, t][:], 1.7, dual_sb[0][:, t, halves[u]], ALU.mult, ALU.add
+                    total[:, t, halves[u]], y[u, t][:], 1.7, dual_plane[t][:, halves[u]], ALU.mult, ALU.add
                 )
         for u in range(2):
             for t in range(2, PACK):
@@ -172,7 +174,7 @@ def tile_picked_yosqp_relax_p_kernel(tc, x_words, x_scales, w1, dual, low, high,
                 total[:, t, S - VECTOR_TAIL : S],
                 y[1, t][:, HALF - VECTOR_TAIL : HALF],
                 1.7,
-                dual_sb[1][:, t - 2, S - VECTOR_TAIL : S],
+                dual_plane[t][:, S - VECTOR_TAIL : S],
                 ALU.mult,
                 ALU.add,
             )
@@ -181,7 +183,6 @@ def tile_picked_yosqp_relax_p_kernel(tc, x_words, x_scales, w1, dual, low, high,
             nc.scalar.activation(linear[:, t, :], total[:, t, :], COPY, scale=rho_sb[:, t : t + 1])
 
         chunks = [slice(STARTS[q], STARTS[q] + WIDTHS[q]) for q in range(CHUNKS)]
-        scaled = sb.tile([P, PACK, S], F32, name="scaled")
         clip = sb.tile([P, PACK, S], F32, name="clip")
         first, rest = chunks[0], slice(STARTS[1], S)
 
@@ -203,6 +204,7 @@ def tile_picked_yosqp_relax_p_kernel(tc, x_words, x_scales, w1, dual, low, high,
             w2_grouped[:].rearrange("p (c i) j -> p c j i", i=4),
             w2_raw[:].rearrange("p j (c i) -> p c j i", i=4),
         )
+        scaled = sb.tile([P, PACK, S], F32, name="scaled", tag="w2_raw")
         w2_codes = sb.tile([P, N], U32, name="w2_codes", align_bytes=64)
         w2_scales = sb.tile([P, N], U8, name="w2_scales", align_bytes=64)
         nc.vector.quantize_mx(

@@ -23,8 +23,8 @@ QUADRANTS = P // 32
 HALF = S // 2
 LIST_COLS = HALF // 16
 OUT_BLOCKS = N // P
-SCALAR_M = 48
-VECTOR_TAIL = 64
+SCALAR_M = (48, 64)
+VECTOR_TAIL = 96
 WIDTHS = (128, 128, 128, 64, 64)
 STARTS = tuple(sum(WIDTHS[:q]) for q in range(len(WIDTHS)))
 CHUNKS = len(WIDTHS)
@@ -47,7 +47,8 @@ def tile_picked_yosqp_relax_p_kernel(tc, x_words, x_scales, w1, dual, low, high,
         dual_second = sb.tile([P, 2, S], F32, name="dual_second")
         dual_plane = [dual_first[0][:], dual_first[1][:], dual_second[:, 0, :], dual_second[:, 1, :]]
         low_sb = [sb.tile([P, 2, S], F32, name="low%d" % pair) for pair in range(2)]
-        high_sb = [sb.tile([P, 2, S], F32, name="high%d" % pair) for pair in range(2)]
+        high_first = sb.tile([P, 2, S], F32, name="high_first")
+        high_second = [sb.tile([P, 2, HALF], F32, name="high_second%d" % u) for u in range(2)]
         w2_raw = sb.tile([P, PACK, N], F32, name="w2_raw", tag="w2_raw")
         lin_sb = sb.tile([P, OUT_BLOCKS, S], F32, name="lin_sb")
 
@@ -85,10 +86,12 @@ def tile_picked_yosqp_relax_p_kernel(tc, x_words, x_scales, w1, dual, low, high,
         nc.sync.dma_start(out=dual_first[1][:], in_=dual_planes[:, 1, :])
         nc.sync.dma_start(out=rho_sb[:], in_=rho.rearrange("(p t) o -> p (t o)", t=PACK))
         load_pair(low_sb, low, 0)
-        load_pair(high_sb, high, 0)
+        high_planes = high.rearrange("(p t) j -> p t j", t=PACK)
+        nc.sync.dma_start(out=high_first[:], in_=high_planes[:, 0:2, :])
         nc.sync.dma_start(out=w2_raw[:], in_=w2.rearrange("(p j) c -> p j c", j=PACK))
         load_pair(low_sb, low, 1)
-        load_pair(high_sb, high, 1)
+        for u in range(2):
+            nc.sync.dma_start(out=high_second[u][:], in_=high_planes[:, 2:PACK, u * HALF : (u + 1) * HALF])
         nc.sync.dma_start(out=lin_sb[:], in_=lin.rearrange("(h p) j -> p h j", p=P))
 
         rho_clip = sb.tile([P, PACK], F32, name="rho_clip")
@@ -103,8 +106,9 @@ def tile_picked_yosqp_relax_p_kernel(tc, x_words, x_scales, w1, dual, low, high,
             grouped = sb.tile([P, PACK, P, PACK], BF16, name="w1_grouped%d" % g, align_bytes=64)
             dst = grouped[:].rearrange("p (a e) m j -> p a m j e", e=2)
             src = w1_raw[g][:].rearrange("p j (m a e) -> p a m j e", a=2, e=2)
-            nc.scalar.copy(dst[:, :, 0:SCALAR_M], src[:, :, 0:SCALAR_M])
-            nc.vector.tensor_copy(dst[:, :, SCALAR_M:P], src[:, :, SCALAR_M:P])
+            share = SCALAR_M[g]
+            nc.scalar.copy(dst[:, :, 0:share], src[:, :, 0:share])
+            nc.vector.tensor_copy(dst[:, :, share:P], src[:, :, share:P])
             codes = sb.tile([P, H], U32, name="w1_codes%d" % g, align_bytes=64)
             scales = sb.tile([P, H], U8, name="w1_scales%d" % g, align_bytes=64)
             nc.vector.quantize_mx(
@@ -184,11 +188,9 @@ def tile_picked_yosqp_relax_p_kernel(tc, x_words, x_scales, w1, dual, low, high,
 
         chunks = [slice(STARTS[q], STARTS[q] + WIDTHS[q]) for q in range(CHUNKS)]
         clip = sb.tile([P, PACK, S], F32, name="clip")
-        first, rest = chunks[0], slice(STARTS[1], S)
 
-        def upper(pair, cols):
-            planes = slice(2 * pair, 2 * pair + 2)
-            nc.vector.tensor_tensor(clip[:, planes, cols], t0[:, planes, cols], high_sb[pair][:, :, cols], ALU.min)
+        def upper(cols, bound):
+            nc.vector.tensor_tensor(clip[:, 2:PACK, cols], t0[:, 2:PACK, cols], bound, ALU.min)
 
         def scale_clip(t, cols):
             nc.scalar.activation(scaled[:, t, cols], clip[:, t, cols], COPY, scale=rho_clip[:, t : t + 1])
@@ -196,7 +198,7 @@ def tile_picked_yosqp_relax_p_kernel(tc, x_words, x_scales, w1, dual, low, high,
         for t in range(2):
             nc.vector.tensor_tensor(t0[:, t, :], t0[:, t, :], low_sb[0][:, t, :], ALU.max)
         for t in range(2):
-            nc.vector.tensor_tensor(clip[:, t, :], t0[:, t, :], high_sb[0][:, t, :], ALU.min)
+            nc.vector.tensor_tensor(clip[:, t, :], t0[:, t, :], high_first[:, t, :], ALU.min)
         nc.vector.tensor_tensor(t0[:, 2:PACK, :], t0[:, 2:PACK, :], low_sb[1][:], ALU.max)
 
         w2_grouped = sb.tile([P, N, PACK], BF16, name="w2_grouped", align_bytes=64)
@@ -210,11 +212,12 @@ def tile_picked_yosqp_relax_p_kernel(tc, x_words, x_scales, w1, dual, low, high,
         nc.vector.quantize_mx(
             out=w2_codes[:].bitcast(FP8X4), scales=w2_scales[:], in_=w2_grouped[:].rearrange("p c j -> p (c j)")
         )
-        upper(1, first)
-        upper(1, rest)
+        upper(chunks[0], high_second[0][:, :, chunks[0]])
+        upper(chunks[1], high_second[0][:, :, chunks[1]])
+        upper(halves[1], high_second[1][:])
         scale_clip(0, slice(0, S))
         scale_clip(1, slice(0, S))
-        for cols in (first, chunks[1], chunks[2], slice(STARTS[3], S)):
+        for cols in (chunks[0], chunks[1], chunks[2], slice(STARTS[3], S)):
             scale_clip(2, cols)
             scale_clip(3, cols)
 

@@ -47,9 +47,8 @@ def tile_picked_yosqp_relax_p_kernel(tc, x_words, x_scales, w1, dual, low, high,
         dual_second = sb.tile([P, 2, S], F32, name="dual_second")
         dual_plane = [dual_first[0][:], dual_first[1][:], dual_second[:, 0, :], dual_second[:, 1, :]]
         low_sb = [sb.tile([P, 2, S], F32, name="low%d" % pair) for pair in range(2)]
-        high_first = sb.tile([P, 2, S], F32, name="high_first")
-        high_second = [sb.tile([P, 2, HALF], F32, name="high_second%d" % u) for u in range(2)]
-        w2_raw = sb.tile([P, PACK, N], F32, name="w2_raw", tag="w2_raw")
+        high_sb = [sb.tile([P, 2, S], F32, name="high%d" % pair) for pair in range(2)]
+        w2_raw = sb.tile([P, PACK, N], F32, name="w2_raw")
         lin_sb = sb.tile([P, OUT_BLOCKS, S], F32, name="lin_sb")
 
         nc.vector.memset(table_scales[:].bitcast(I32), 0)
@@ -86,12 +85,10 @@ def tile_picked_yosqp_relax_p_kernel(tc, x_words, x_scales, w1, dual, low, high,
         nc.sync.dma_start(out=dual_first[1][:], in_=dual_planes[:, 1, :])
         nc.sync.dma_start(out=rho_sb[:], in_=rho.rearrange("(p t) o -> p (t o)", t=PACK))
         load_pair(low_sb, low, 0)
-        high_planes = high.rearrange("(p t) j -> p t j", t=PACK)
-        nc.sync.dma_start(out=high_first[:], in_=high_planes[:, 0:2, :])
-        nc.sync.dma_start(out=w2_raw[:], in_=w2.rearrange("(p j) c -> p j c", j=PACK))
+        load_pair(high_sb, high, 0)
         load_pair(low_sb, low, 1)
-        for u in range(2):
-            nc.sync.dma_start(out=high_second[u][:], in_=high_planes[:, 2:PACK, u * HALF : (u + 1) * HALF])
+        load_pair(high_sb, high, 1)
+        nc.sync.dma_start(out=w2_raw[:], in_=w2.rearrange("(p j) c -> p j c", j=PACK))
         nc.sync.dma_start(out=lin_sb[:], in_=lin.rearrange("(h p) j -> p h j", p=P))
 
         rho_clip = sb.tile([P, PACK], F32, name="rho_clip")
@@ -187,42 +184,46 @@ def tile_picked_yosqp_relax_p_kernel(tc, x_words, x_scales, w1, dual, low, high,
             nc.scalar.activation(linear[:, t, :], total[:, t, :], COPY, scale=rho_sb[:, t : t + 1])
 
         chunks = [slice(STARTS[q], STARTS[q] + WIDTHS[q]) for q in range(CHUNKS)]
-        clip = sb.tile([P, PACK, S], F32, name="clip")
+        scaled = sb.tile([P, PACK, S], F32, name="scaled")
 
-        def upper(cols, bound):
-            nc.vector.tensor_tensor(clip[:, 2:PACK, cols], t0[:, 2:PACK, cols], bound, ALU.min)
-
-        def scale_clip(t, cols):
-            nc.scalar.activation(scaled[:, t, cols], clip[:, t, cols], COPY, scale=rho_clip[:, t : t + 1])
+        def scale_clip(t, cols, clip):
+            nc.scalar.activation(scaled[:, t, cols], clip, COPY, scale=rho_clip[:, t : t + 1])
 
         for t in range(2):
             nc.vector.tensor_tensor(t0[:, t, :], t0[:, t, :], low_sb[0][:, t, :], ALU.max)
+        clip_first = sb.tile([P, 2, S], F32, name="clip_first")
         for t in range(2):
-            nc.vector.tensor_tensor(clip[:, t, :], t0[:, t, :], high_first[:, t, :], ALU.min)
-        nc.vector.tensor_tensor(t0[:, 2:PACK, :], t0[:, 2:PACK, :], low_sb[1][:], ALU.max)
-
-        w2_grouped = sb.tile([P, N, PACK], BF16, name="w2_grouped", align_bytes=64)
-        nc.scalar.copy(
-            w2_grouped[:].rearrange("p (c i) j -> p c j i", i=4),
-            w2_raw[:].rearrange("p j (c i) -> p c j i", i=4),
-        )
-        scaled = sb.tile([P, PACK, S], F32, name="scaled", tag="w2_raw")
+            nc.vector.tensor_tensor(clip_first[:, t, :], t0[:, t, :], high_sb[0][:, t, :], ALU.min)
+            scale_clip(t, slice(0, S), clip_first[:, t, :])
+        for cols in halves:
+            nc.vector.tensor_tensor(t0[:, 2:PACK, cols], t0[:, 2:PACK, cols], low_sb[1][:, :, cols], ALU.max)
+        w2_grouped = []
+        for n in range(S // P):
+            cols = slice(n * P, (n + 1) * P)
+            clip = sb.tile([P, 2, P], F32, name="clip%d" % n, tag="clip%d" % n, align_bytes=64)
+            nc.vector.tensor_tensor(clip[:], t0[:, 2:PACK, cols], high_sb[1][:, :, cols], ALU.min)
+            for e in range(2):
+                scale_clip(2 + e, cols, clip[:, e, :])
+            h = n - 1
+            if 0 <= h < OUT_BLOCKS:
+                grouped = sb.tile([P, P, PACK], BF16, name="w2_grouped%d" % h, tag="clip%d" % n, align_bytes=64)
+                nc.scalar.copy(
+                    grouped[:].rearrange("p (c i) j -> p c j i", i=4),
+                    w2_raw[:, :, h * P : (h + 1) * P].rearrange("p j (c i) -> p c j i", i=4),
+                )
+                w2_grouped.append(grouped)
         w2_codes = sb.tile([P, N], U32, name="w2_codes", align_bytes=64)
         w2_scales = sb.tile([P, N], U8, name="w2_scales", align_bytes=64)
-        nc.vector.quantize_mx(
-            out=w2_codes[:].bitcast(FP8X4), scales=w2_scales[:], in_=w2_grouped[:].rearrange("p c j -> p (c j)")
-        )
-        upper(chunks[0], high_second[0][:, :, chunks[0]])
-        upper(chunks[1], high_second[0][:, :, chunks[1]])
-        upper(halves[1], high_second[1][:])
-        scale_clip(0, slice(0, S))
-        scale_clip(1, slice(0, S))
-        for cols in (chunks[0], chunks[1], chunks[2], slice(STARTS[3], S)):
-            scale_clip(2, cols)
-            scale_clip(3, cols)
+
+        def quantize_w2(h):
+            nc.vector.quantize_mx(
+                out=w2_codes[:, h * P : (h + 1) * P].bitcast(FP8X4),
+                scales=w2_scales[:, h * P : (h + 1) * P],
+                in_=w2_grouped[h][:].rearrange("p c j -> p (c j)"),
+            )
 
         out_blocks = out.rearrange("(h p) j -> p h j", p=P)
-        rr, acc = {}, {}
+        rr, codes, scales, acc = {}, {}, {}, {}
 
         def residual(q):
             rr[q] = sb.tile([P, WIDTHS[q], PACK], BF16, name="rr%d" % q, align_bytes=64)
@@ -233,20 +234,22 @@ def tile_picked_yosqp_relax_p_kernel(tc, x_words, x_scales, w1, dual, low, high,
                 ALU.subtract,
             )
 
-        def product(q):
-            codes = sb.tile([P, WIDTHS[q]], U32, name="rr_codes%d" % q, align_bytes=64)
-            scales = sb.tile([P, WIDTHS[q]], U8, name="rr_scales%d" % q, align_bytes=64)
+        def quantize(q):
+            codes[q] = sb.tile([P, WIDTHS[q]], U32, name="rr_codes%d" % q, align_bytes=64)
+            scales[q] = sb.tile([P, WIDTHS[q]], U8, name="rr_scales%d" % q, align_bytes=64)
             nc.vector.quantize_mx(
-                out=codes[:].bitcast(FP8X4), scales=scales[:], in_=rr[q][:].rearrange("p j t -> p (j t)")
+                out=codes[q][:].bitcast(FP8X4), scales=scales[q][:], in_=rr[q][:].rearrange("p j t -> p (j t)")
             )
+
+        def product(q):
             acc[q] = ps.tile([P, OUT_BLOCKS, WIDTHS[q]], F32, name="acc%d" % q, tag="bank%d" % q)
             for h in range(OUT_BLOCKS):
                 nc.tensor.matmul_mx(
                     out=acc[q][:, h, :],
                     lhsT=w2_codes[:, h * P : (h + 1) * P].bitcast(FP8X4),
                     lhsT_scale=w2_scales[:, h * P : (h + 1) * P],
-                    rhs=codes[:].bitcast(FP8X4),
-                    rhs_scale=scales[:],
+                    rhs=codes[q][:].bitcast(FP8X4),
+                    rhs_scale=scales[q][:],
                     start=True,
                     stop=True,
                 )
@@ -256,10 +259,19 @@ def tile_picked_yosqp_relax_p_kernel(tc, x_words, x_scales, w1, dual, low, high,
             nc.vector.tensor_tensor(res[:], acc[q][:], lin_sb[:, :, chunks[q]], ALU.add)
             nc.sync.dma_start(out=out_blocks[:, :, chunks[q]], in_=res[:])
 
-        for step in range(CHUNKS + FINISH_LAG):
-            if step < CHUNKS:
-                residual(step)
-            if PRODUCT_LAG <= step < CHUNKS + PRODUCT_LAG:
-                product(step - PRODUCT_LAG)
-            if step >= FINISH_LAG:
-                finish(step - FINISH_LAG)
+        residual(0)
+        for h in range(OUT_BLOCKS):
+            residual(1 + h)
+            quantize(h)
+            quantize_w2(h)
+        product(0)
+        product(1)
+        for q in range(OUT_BLOCKS + 1, CHUNKS):
+            residual(q)
+            quantize(q - 1)
+            product(q - 1)
+        finish(0)
+        quantize(CHUNKS - 1)
+        product(CHUNKS - 1)
+        for q in range(1, CHUNKS):
+            finish(q)

@@ -1,6 +1,7 @@
 from contextlib import ExitStack
 
 import concourse.mybir as mybir
+from concourse.masks import make_identity
 
 K, T, S, H, N = 1024, 2048, 512, 512, 256
 FLOPS = 2 * K * H * S + 2 * H * N * S
@@ -46,7 +47,7 @@ def tile_picked_yosqp_relax_p_kernel(tc, x_words, x_scales, w1, dual, low, high,
         dual_first = [sb.tile([P, S], F32, name="dual%d" % t) for t in range(2)]
         dual_second = sb.tile([P, 2, S], F32, name="dual_second")
         dual_plane = [dual_first[0][:], dual_first[1][:], dual_second[:, 0, :], dual_second[:, 1, :]]
-        low_sb = [sb.tile([P, 2, S], F32, name="low%d" % pair) for pair in range(2)]
+        low_sb = [sb.tile([P, 2, S], F32, name="low%d" % pair, tag="low%d" % pair, align_bytes=64) for pair in range(2)]
         high_sb = [sb.tile([P, 2, S], F32, name="high%d" % pair) for pair in range(2)]
         w2_raw = sb.tile([P, PACK, N], F32, name="w2_raw")
         lin_sb = sb.tile([P, OUT_BLOCKS, S], F32, name="lin_sb")
@@ -84,15 +85,19 @@ def tile_picked_yosqp_relax_p_kernel(tc, x_words, x_scales, w1, dual, low, high,
         nc.sync.dma_start(out=dual_second[:], in_=dual_planes[:, 2:PACK, :])
         nc.sync.dma_start(out=dual_first[1][:], in_=dual_planes[:, 1, :])
         nc.sync.dma_start(out=rho_sb[:], in_=rho.rearrange("(p t) o -> p (t o)", t=PACK))
+        nc.sync.dma_start(out=w2_raw[:], in_=w2.rearrange("(p j) c -> p j c", j=PACK))
         load_pair(low_sb, low, 0)
         load_pair(high_sb, high, 0)
         load_pair(low_sb, low, 1)
         load_pair(high_sb, high, 1)
-        nc.sync.dma_start(out=w2_raw[:], in_=w2.rearrange("(p j) c -> p j c", j=PACK))
         nc.sync.dma_start(out=lin_sb[:], in_=lin.rearrange("(h p) j -> p h j", p=P))
 
         rho_clip = sb.tile([P, PACK], F32, name="rho_clip")
         nc.scalar.activation(rho_clip[:], rho_sb[:], COPY, scale=3.0)
+        rho_neg = sb.tile([P, PACK], F32, name="rho_neg")
+        nc.scalar.activation(rho_neg[:], rho_sb[:], COPY, scale=-1.0)
+        identity = sb.tile([P, P], F32, name="identity")
+        make_identity(nc, identity[:])
 
         def gather_half(name, dtype, window, u):
             picked = sb.tile([P, HALF], dtype, name="%s_%d" % (name, u), align_bytes=64)
@@ -180,8 +185,34 @@ def tile_picked_yosqp_relax_p_kernel(tc, x_words, x_scales, w1, dual, low, high,
                 ALU.add,
             )
         linear = sb.tile([P, PACK, S], F32, name="linear")
+        w2_grouped = []
+
+        def round_w2(h):
+            grouped = sb.tile([P, P, PACK], BF16, name="w2_grouped%d" % h, align_bytes=64)
+            nc.scalar.copy(
+                grouped[:].rearrange("p (c i) j -> p c j i", i=4),
+                w2_raw[:, :, h * P : (h + 1) * P].rearrange("p j (c i) -> p c j i", i=4),
+            )
+            w2_grouped.append(grouped)
+
+        turned = [ps.tile([P, 2, P], F32, name="turned%d" % a, tag="bank%d" % (5 + 2 * a)) for a in range(2)]
+        back = ps.tile([P, 2, P], F32, name="back", tag="bank6")
+
+        def add_turned(t, src, start=False, stop=False):
+            nc.tensor.matmul(
+                turned[t // 2][:, t % 2, :], src[:, t, 0:P], identity[:], start=start, stop=stop, is_transpose=True
+            )
+
+        def turn_back(a, tag):
+            pairs = sb.tile([P, P, 2], BF16, name="pairs%d" % a, tag=tag)
+            nc.scalar.copy(pairs[:], turned[a][:].rearrange("j e p -> j p e"))
+            nc.tensor.transpose(back[:, a, :], pairs[:].rearrange("j p e -> j (p e)").bitcast(F32), identity[:])
+
         for t in range(PACK):
-            nc.scalar.activation(linear[:, t, :], total[:, t, :], COPY, scale=rho_sb[:, t : t + 1])
+            nc.scalar.activation(linear[:, t, :], total[:, t, :], COPY, scale=rho_neg[:, t : t + 1])
+            add_turned(t, linear, start=t % 2 == 0)
+            if t % 2 == 1:
+                round_w2(t // 2)
 
         chunks = [slice(STARTS[q], STARTS[q] + WIDTHS[q]) for q in range(CHUNKS)]
         scaled = sb.tile([P, PACK, S], F32, name="scaled")
@@ -195,24 +226,25 @@ def tile_picked_yosqp_relax_p_kernel(tc, x_words, x_scales, w1, dual, low, high,
         for t in range(2):
             nc.vector.tensor_tensor(clip_first[:, t, :], t0[:, t, :], high_sb[0][:, t, :], ALU.min)
             scale_clip(t, slice(0, S), clip_first[:, t, :])
+            add_turned(t, scaled, stop=t == 1)
         for cols in halves:
             nc.vector.tensor_tensor(t0[:, 2:PACK, cols], t0[:, 2:PACK, cols], low_sb[1][:, :, cols], ALU.max)
-        w2_grouped = []
         for n in range(S // P):
             cols = slice(n * P, (n + 1) * P)
-            clip = sb.tile([P, 2, P], F32, name="clip%d" % n, tag="clip%d" % n, align_bytes=64)
+            clip = sb.tile([P, 2, P], F32, name="clip%d" % n, tag="clip%d" % n)
             nc.vector.tensor_tensor(clip[:], t0[:, 2:PACK, cols], high_sb[1][:, :, cols], ALU.min)
             for e in range(2):
                 scale_clip(2 + e, cols, clip[:, e, :])
-            h = n - 1
-            if 0 <= h < OUT_BLOCKS:
-                grouped = sb.tile([P, P, PACK], BF16, name="w2_grouped%d" % h, tag="clip%d" % n, align_bytes=64)
-                nc.scalar.copy(
-                    grouped[:].rearrange("p (c i) j -> p c j i", i=4),
-                    w2_raw[:, :, h * P : (h + 1) * P].rearrange("p j (c i) -> p c j i", i=4),
-                )
-                w2_grouped.append(grouped)
-        w2_codes = sb.tile([P, N], U32, name="w2_codes", align_bytes=64)
+                if n == 0:
+                    add_turned(2 + e, scaled, stop=e == 1)
+            if n < 2:
+                turn_back(n, "clip%d" % n)
+        rr_first = sb.tile([P, P, PACK], BF16, name="rr0", align_bytes=64)
+        nc.scalar.copy(
+            rr_first[:].rearrange("p j t -> p (j t)").bitcast(F32).rearrange("p (j a) -> p j a", a=2),
+            back[:].rearrange("p a j -> p j a"),
+        )
+        w2_codes = sb.tile([P, N], U32, name="w2_codes", tag="low1", align_bytes=64)
         w2_scales = sb.tile([P, N], U8, name="w2_scales", align_bytes=64)
 
         def quantize_w2(h):
@@ -223,7 +255,7 @@ def tile_picked_yosqp_relax_p_kernel(tc, x_words, x_scales, w1, dual, low, high,
             )
 
         out_blocks = out.rearrange("(h p) j -> p h j", p=P)
-        rr, codes, scales, acc = {}, {}, {}, {}
+        rr, codes, scales, acc = {0: rr_first}, {}, {}, {}
 
         def residual(q):
             rr[q] = sb.tile([P, WIDTHS[q], PACK], BF16, name="rr%d" % q, align_bytes=64)
@@ -231,7 +263,7 @@ def tile_picked_yosqp_relax_p_kernel(tc, x_words, x_scales, w1, dual, low, high,
                 rr[q][:].rearrange("p (c i) t -> p c t i", i=2),
                 scaled[:, :, chunks[q]].rearrange("p t (c i) -> p c t i", i=2),
                 linear[:, :, chunks[q]].rearrange("p t (c i) -> p c t i", i=2),
-                ALU.subtract,
+                ALU.add,
             )
 
         def quantize(q):
@@ -259,19 +291,16 @@ def tile_picked_yosqp_relax_p_kernel(tc, x_words, x_scales, w1, dual, low, high,
             nc.vector.tensor_tensor(res[:], acc[q][:], lin_sb[:, :, chunks[q]], ALU.add)
             nc.sync.dma_start(out=out_blocks[:, :, chunks[q]], in_=res[:])
 
-        residual(0)
-        for h in range(OUT_BLOCKS):
-            residual(1 + h)
-            quantize(h)
-            quantize_w2(h)
-        product(0)
-        product(1)
-        for q in range(OUT_BLOCKS + 1, CHUNKS):
+        quantize_w2(0)
+        quantize_w2(1)
+        residual(1)
+        for q in range(2, CHUNKS):
             residual(q)
             quantize(q - 1)
             product(q - 1)
-        finish(0)
+        quantize(0)
+        product(0)
         quantize(CHUNKS - 1)
         product(CHUNKS - 1)
-        for q in range(1, CHUNKS):
+        for q in (1, 2, 3, 0, 4):
             finish(q)

@@ -26,7 +26,7 @@ LIST_COLS = HALF // 16
 OUT_BLOCKS = N // P
 SCALAR_M = (48, 64)
 VECTOR_TAIL = 96
-WIDTHS = (128, 128, 128, 64, 64)
+WIDTHS = (128, 128, 128, 128)
 STARTS = tuple(sum(WIDTHS[:q]) for q in range(len(WIDTHS)))
 CHUNKS = len(WIDTHS)
 PRODUCT_LAG = 1
@@ -294,13 +294,13 @@ def tile_picked_yosqp_relax_p_kernel(tc, x_words, x_scales, w1, dual, low, high,
         quantize_w2(0)
         quantize_w2(1)
         residual(1)
-        for q in range(2, CHUNKS):
-            residual(q)
-            quantize(q - 1)
-            product(q - 1)
-        quantize(0)
-        product(0)
-        quantize(CHUNKS - 1)
-        product(CHUNKS - 1)
-        for q in (1, 2, 3, 0, 4):
+        residual(2)
+        for q in (1, 2):
+            quantize(q)
+            product(q)
+        residual(3)
+        for q in (0, 3):
+            quantize(q)
+            product(q)
+        for q in (1, 2, 0, 3):
             finish(q)

@@ -47,9 +47,11 @@ def tile_picked_yosqp_relax_p_kernel(tc, x_words, x_scales, w1, dual, low, high,
         dual_first = [sb.tile([P, S], F32, name="dual%d" % t) for t in range(2)]
         dual_second = sb.tile([P, 2, S], F32, name="dual_second")
         dual_plane = [dual_first[0][:], dual_first[1][:], dual_second[:, 0, :], dual_second[:, 1, :]]
-        low_sb = [sb.tile([P, 2, S], F32, name="low%d" % pair, tag="low%d" % pair, align_bytes=64) for pair in range(2)]
-        high_sb = [sb.tile([P, 2, S], F32, name="high%d" % pair) for pair in range(2)]
-        w2_raw = sb.tile([P, PACK, N], F32, name="w2_raw")
+        low_first = [sb.tile([P, S], F32, name="low_first%d" % t, tag="low_first%d" % t, align_bytes=64) for t in range(2)]
+        high_first = sb.tile([P, 2, S], F32, name="high_first")
+        low_second = [sb.tile([P, 2, HALF], F32, name="low_second%d" % u, tag="low_second%d" % u, align_bytes=64) for u in range(2)]
+        high_second = [sb.tile([P, 2, HALF], F32, name="high_second%d" % u) for u in range(2)]
+        w2_raw = sb.tile([P, PACK, N], F32, name="w2_raw", tag="w2_raw")
         lin_sb = sb.tile([P, OUT_BLOCKS, S], F32, name="lin_sb")
 
         nc.vector.memset(table_scales[:].bitcast(I32), 0)
@@ -83,19 +85,24 @@ def tile_picked_yosqp_relax_p_kernel(tc, x_words, x_scales, w1, dual, low, high,
         dual_planes = dual.rearrange("(p t) j -> p t j", t=PACK)
         nc.sync.dma_start(out=dual_first[0][:], in_=dual_planes[:, 0, :])
         nc.sync.dma_start(out=dual_second[:], in_=dual_planes[:, 2:PACK, :])
-        nc.sync.dma_start(out=dual_first[1][:], in_=dual_planes[:, 1, :])
         nc.sync.dma_start(out=rho_sb[:], in_=rho.rearrange("(p t) o -> p (t o)", t=PACK))
         nc.sync.dma_start(out=w2_raw[:], in_=w2.rearrange("(p j) c -> p j c", j=PACK))
-        load_pair(low_sb, low, 0)
-        load_pair(high_sb, high, 0)
-        load_pair(low_sb, low, 1)
-        load_pair(high_sb, high, 1)
+        nc.sync.dma_start(out=dual_first[1][:], in_=dual_planes[:, 1, :])
+        for t in range(2):
+            nc.sync.dma_start(out=low_first[t][:], in_=low.rearrange("(p t) j -> p t j", t=PACK)[:, t, :])
+        load_pair([high_first], high, 0)
+        for u in range(2):
+            for tiles, src in ((low_second, low), (high_second, high)):
+                planes = src.rearrange("(p t) j -> p t j", t=PACK)
+                nc.sync.dma_start(out=tiles[u][:], in_=planes[:, 2:PACK, u * HALF : (u + 1) * HALF])
         nc.sync.dma_start(out=lin_sb[:], in_=lin.rearrange("(h p) j -> p h j", p=P))
 
         rho_clip = sb.tile([P, PACK], F32, name="rho_clip")
         nc.scalar.activation(rho_clip[:], rho_sb[:], COPY, scale=3.0)
         rho_neg = sb.tile([P, PACK], F32, name="rho_neg")
         nc.scalar.activation(rho_neg[:], rho_sb[:], COPY, scale=-1.0)
+        rho_y = sb.tile([P, PACK], F32, name="rho_y")
+        nc.scalar.activation(rho_y[:], rho_sb[:], COPY, scale=-1.7)
         identity = sb.tile([P, P], F32, name="identity")
         make_identity(nc, identity[:])
 
@@ -160,31 +167,27 @@ def tile_picked_yosqp_relax_p_kernel(tc, x_words, x_scales, w1, dual, low, high,
             )
 
         total = sb.tile([P, PACK, S], F32, name="total")
-        for u, width in enumerate((HALF, HALF - VECTOR_TAIL)):
-            y_term = sb.tile([P, 2, width], F32, name="y_term%d" % u)
-            cols = slice(u * HALF, u * HALF + width)
-            for e in range(2):
-                nc.scalar.activation(y_term[:, e, :], y[u, 2 + e][:, 0:width], COPY, scale=1.7)
-            nc.gpsimd.tensor_tensor(total[:, 2:PACK, cols], y_term[:], dual_second[:, :, cols], ALU.add)
-        for t in range(2):
-            for u in range(2):
+        for e in range(2):
+            nc.scalar.activation(total[:, 2 + e, halves[0]], y[0, 2 + e][:], COPY, scale=1.7)
+        nc.gpsimd.tensor_tensor(total[:, 2:PACK, P:HALF], total[:, 2:PACK, P:HALF], dual_second[:, :, P:HALF], ALU.add)
+        y_term = sb.tile([P, 2, HALF], F32, name="y_term", tag="y_term", align_bytes=64)
+        for e in range(2):
+            nc.scalar.activation(y_term[:, e, :], y[1, 2 + e][:], COPY, scale=1.7)
+        nc.gpsimd.tensor_tensor(total[:, 2:PACK, halves[1]], y_term[:], dual_second[:, :, halves[1]], ALU.add)
+
+        def first_plane(t):
+            for u, skip in enumerate((P, 0)):
                 make_t0(u, t)
+                cols = slice(u * HALF + skip, (u + 1) * HALF)
                 nc.vector.scalar_tensor_tensor(
-                    total[:, t, halves[u]], y[u, t][:], 1.7, dual_plane[t][:, halves[u]], ALU.mult, ALU.add
+                    total[:, t, cols], y[u, t][:, skip:HALF], 1.7, dual_plane[t][:, cols], ALU.mult, ALU.add
                 )
+
+        first_plane(0)
         for u in range(2):
             for t in range(2, PACK):
                 make_t0(u, t)
-        for t in range(2, PACK):
-            nc.vector.scalar_tensor_tensor(
-                total[:, t, S - VECTOR_TAIL : S],
-                y[1, t][:, HALF - VECTOR_TAIL : HALF],
-                1.7,
-                dual_plane[t][:, S - VECTOR_TAIL : S],
-                ALU.mult,
-                ALU.add,
-            )
-        linear = sb.tile([P, PACK, S], F32, name="linear")
+        first_plane(1)
         w2_grouped = []
 
         def round_w2(h):
@@ -194,9 +197,6 @@ def tile_picked_yosqp_relax_p_kernel(tc, x_words, x_scales, w1, dual, low, high,
                 w2_raw[:, :, h * P : (h + 1) * P].rearrange("p j (c i) -> p c j i", i=4),
             )
             w2_grouped.append(grouped)
-
-        turned = [ps.tile([P, 2, P], F32, name="turned%d" % a, tag="bank%d" % (5 + 2 * a)) for a in range(2)]
-        back = ps.tile([P, 2, P], F32, name="back", tag="bank6")
 
         def add_turned(t, src, start=False, stop=False):
             nc.tensor.matmul(
@@ -208,43 +208,6 @@ def tile_picked_yosqp_relax_p_kernel(tc, x_words, x_scales, w1, dual, low, high,
             nc.scalar.copy(pairs[:], turned[a][:].rearrange("j e p -> j p e"))
             nc.tensor.transpose(back[:, a, :], pairs[:].rearrange("j p e -> j (p e)").bitcast(F32), identity[:])
 
-        for t in range(PACK):
-            nc.scalar.activation(linear[:, t, :], total[:, t, :], COPY, scale=rho_neg[:, t : t + 1])
-            add_turned(t, linear, start=t % 2 == 0)
-            if t % 2 == 1:
-                round_w2(t // 2)
-
-        chunks = [slice(STARTS[q], STARTS[q] + WIDTHS[q]) for q in range(CHUNKS)]
-        scaled = sb.tile([P, PACK, S], F32, name="scaled")
-
-        def scale_clip(t, cols, clip):
-            nc.scalar.activation(scaled[:, t, cols], clip, COPY, scale=rho_clip[:, t : t + 1])
-
-        for t in range(2):
-            nc.vector.tensor_tensor(t0[:, t, :], t0[:, t, :], low_sb[0][:, t, :], ALU.max)
-        clip_first = sb.tile([P, 2, S], F32, name="clip_first")
-        for t in range(2):
-            nc.vector.tensor_tensor(clip_first[:, t, :], t0[:, t, :], high_sb[0][:, t, :], ALU.min)
-            scale_clip(t, slice(0, S), clip_first[:, t, :])
-            add_turned(t, scaled, stop=t == 1)
-        for cols in halves:
-            nc.vector.tensor_tensor(t0[:, 2:PACK, cols], t0[:, 2:PACK, cols], low_sb[1][:, :, cols], ALU.max)
-        for n in range(S // P):
-            cols = slice(n * P, (n + 1) * P)
-            clip = sb.tile([P, 2, P], F32, name="clip%d" % n, tag="clip%d" % n)
-            nc.vector.tensor_tensor(clip[:], t0[:, 2:PACK, cols], high_sb[1][:, :, cols], ALU.min)
-            for e in range(2):
-                scale_clip(2 + e, cols, clip[:, e, :])
-                if n == 0:
-                    add_turned(2 + e, scaled, stop=e == 1)
-            if n < 2:
-                turn_back(n, "clip%d" % n)
-        rr_first = sb.tile([P, P, PACK], BF16, name="rr0", align_bytes=64)
-        nc.scalar.copy(
-            rr_first[:].rearrange("p j t -> p (j t)").bitcast(F32).rearrange("p (j a) -> p j a", a=2),
-            back[:].rearrange("p a j -> p j a"),
-        )
-        w2_codes = sb.tile([P, N], U32, name="w2_codes", tag="low1", align_bytes=64)
         w2_scales = sb.tile([P, N], U8, name="w2_scales", align_bytes=64)
 
         def quantize_w2(h):
@@ -253,6 +216,62 @@ def tile_picked_yosqp_relax_p_kernel(tc, x_words, x_scales, w1, dual, low, high,
                 scales=w2_scales[:, h * P : (h + 1) * P],
                 in_=w2_grouped[h][:].rearrange("p c j -> p (c j)"),
             )
+
+        for h in range(OUT_BLOCKS):
+            round_w2(h)
+        linear = sb.tile([P, PACK, S], F32, name="linear", tag="w2_raw")
+        dual_term = sb.tile([P, PACK, P], F32, name="dual_term")
+        for t in (0, 2, 3, 1):
+            nc.scalar.activation(dual_term[:, t, :], dual_plane[t][:, 0:P], COPY, scale=rho_neg[:, t : t + 1])
+            if t < 2:
+                nc.scalar.activation(linear[:, t, 0:P], y[0, t][:, 0:P], COPY, scale=rho_y[:, t : t + 1])
+        for t in range(PACK):
+            cols = slice(P if t < 2 else 0, S)
+            nc.scalar.activation(linear[:, t, cols], total[:, t, cols], COPY, scale=rho_neg[:, t : t + 1])
+        turned = [ps.tile([P, 2, P], F32, name="turned%d" % a, tag="bank%d" % (5 + 2 * a)) for a in range(2)]
+        back = ps.tile([P, 2, P], F32, name="back", tag="bank6")
+        for t in range(PACK):
+            add_turned(t, dual_term, start=t % 2 == 0)
+            add_turned(t, linear)
+
+        chunks = [slice(STARTS[q], STARTS[q] + WIDTHS[q]) for q in range(CHUNKS)]
+        scaled = sb.tile([P, PACK, S], F32, name="scaled")
+
+        def scale_clip(t, cols, clip):
+            nc.scalar.activation(scaled[:, t, cols], clip, COPY, scale=rho_clip[:, t : t + 1])
+
+        for t in range(2):
+            nc.vector.tensor_tensor(t0[:, t, :], t0[:, t, :], low_first[t][:], ALU.max)
+        w2_codes = sb.tile([P, N], U32, name="w2_codes", tag="low_first0", align_bytes=64)
+        for h in range(OUT_BLOCKS):
+            quantize_w2(h)
+        clip_first = sb.tile([P, 2, S], F32, name="clip_first")
+        for t in range(2):
+            nc.vector.tensor_tensor(clip_first[:, t, :], t0[:, t, :], high_first[:, t, :], ALU.min)
+            scale_clip(t, slice(0, S), clip_first[:, t, :])
+            add_turned(t, scaled, stop=t == 1)
+        for n in range(S // P):
+            cols = slice(n * P, (n + 1) * P)
+            part = slice(n % 2 * P, (n % 2 + 1) * P)
+            if n % 2 == 0:
+                for m in range(2):
+                    both = chunks[n + m]
+                    nc.vector.tensor_tensor(
+                        t0[:, 2:PACK, both], t0[:, 2:PACK, both], low_second[n // 2][:, :, m * P : (m + 1) * P], ALU.max
+                    )
+            clip = sb.tile([P, 2, P], F32, name="clip%d" % n, tag="clip%d" % n)
+            nc.vector.tensor_tensor(clip[:], t0[:, 2:PACK, cols], high_second[n // 2][:, :, part], ALU.min)
+            for e in range(2):
+                scale_clip(2 + e, cols, clip[:, e, :])
+                if n == 0:
+                    add_turned(2 + e, scaled, stop=e == 1)
+            if n in (0, 2):
+                turn_back(n // 2, "clip%d" % n)
+        rr_first = sb.tile([P, P, PACK], BF16, name="rr0", align_bytes=64)
+        nc.scalar.copy(
+            rr_first[:].rearrange("p j t -> p (j t)").bitcast(F32).rearrange("p (j a) -> p j a", a=2),
+            back[:].rearrange("p a j -> p j a"),
+        )
 
         out_blocks = out.rearrange("(h p) j -> p h j", p=P)
         rr, codes, scales, acc = {0: rr_first}, {}, {}, {}
@@ -291,8 +310,6 @@ def tile_picked_yosqp_relax_p_kernel(tc, x_words, x_scales, w1, dual, low, high,
             nc.vector.tensor_tensor(res[:], acc[q][:], lin_sb[:, :, chunks[q]], ALU.add)
             nc.sync.dma_start(out=out_blocks[:, :, chunks[q]], in_=res[:])
 
-        quantize_w2(0)
-        quantize_w2(1)
         residual(1)
         residual(2)
         for q in (1, 2):

@@ -25,12 +25,7 @@ HALF = S // 2
 LIST_COLS = HALF // 16
 OUT_BLOCKS = N // P
 SCALAR_M = (48, 64)
-VECTOR_TAIL = 96
-WIDTHS = (128, 128, 128, 128)
-STARTS = tuple(sum(WIDTHS[:q]) for q in range(len(WIDTHS)))
-CHUNKS = len(WIDTHS)
-PRODUCT_LAG = 1
-FINISH_LAG = 4
+CHUNKS = S // P
 
 
 def tile_picked_yosqp_relax_p_kernel(tc, x_words, x_scales, w1, dual, low, high, rho, w2, lin, offs, out):
@@ -71,9 +66,8 @@ def tile_picked_yosqp_relax_p_kernel(tc, x_words, x_scales, w1, dual, low, high,
         def load_words(g):
             nc.sync.dma_start(out=table[g][:].bitcast(I32), in_=x_words[g].rearrange("p n t -> p (n t)").bitcast(I32))
 
-        def load_pair(tiles, src, pair):
-            planes = src.rearrange("(p t) j -> p t j", t=PACK)
-            nc.sync.dma_start(out=tiles[pair][:], in_=planes[:, 2 * pair : 2 * pair + 2, :])
+        def planes_of(src):
+            return src.rearrange("(p t) j -> p t j", t=PACK)
 
         load_w1(0)
         nc.sync.dma_start(offsets[:], offs)
@@ -82,19 +76,18 @@ def tile_picked_yosqp_relax_p_kernel(tc, x_words, x_scales, w1, dual, low, high,
         load_scales((2, 3))
         load_w1(1)
         load_words(1)
-        dual_planes = dual.rearrange("(p t) j -> p t j", t=PACK)
+        dual_planes = planes_of(dual)
         nc.sync.dma_start(out=dual_first[0][:], in_=dual_planes[:, 0, :])
         nc.sync.dma_start(out=dual_second[:], in_=dual_planes[:, 2:PACK, :])
         nc.sync.dma_start(out=rho_sb[:], in_=rho.rearrange("(p t) o -> p (t o)", t=PACK))
         nc.sync.dma_start(out=w2_raw[:], in_=w2.rearrange("(p j) c -> p j c", j=PACK))
         nc.sync.dma_start(out=dual_first[1][:], in_=dual_planes[:, 1, :])
         for t in range(2):
-            nc.sync.dma_start(out=low_first[t][:], in_=low.rearrange("(p t) j -> p t j", t=PACK)[:, t, :])
-        load_pair([high_first], high, 0)
+            nc.sync.dma_start(out=low_first[t][:], in_=planes_of(low)[:, t, :])
+        nc.sync.dma_start(out=high_first[:], in_=planes_of(high)[:, 0:2, :])
         for u in range(2):
             for tiles, src in ((low_second, low), (high_second, high)):
-                planes = src.rearrange("(p t) j -> p t j", t=PACK)
-                nc.sync.dma_start(out=tiles[u][:], in_=planes[:, 2:PACK, u * HALF : (u + 1) * HALF])
+                nc.sync.dma_start(out=tiles[u][:], in_=planes_of(src)[:, 2:PACK, u * HALF : (u + 1) * HALF])
         nc.sync.dma_start(out=lin_sb[:], in_=lin.rearrange("(h p) j -> p h j", p=P))
 
         rho_clip = sb.tile([P, PACK], F32, name="rho_clip")
@@ -234,7 +227,7 @@ def tile_picked_yosqp_relax_p_kernel(tc, x_words, x_scales, w1, dual, low, high,
             add_turned(t, dual_term, start=t % 2 == 0)
             add_turned(t, linear)
 
-        chunks = [slice(STARTS[q], STARTS[q] + WIDTHS[q]) for q in range(CHUNKS)]
+        chunks = [slice(q * P, (q + 1) * P) for q in range(CHUNKS)]
         scaled = sb.tile([P, PACK, S], F32, name="scaled")
 
         def scale_clip(t, cols, clip):
@@ -250,8 +243,7 @@ def tile_picked_yosqp_relax_p_kernel(tc, x_words, x_scales, w1, dual, low, high,
             nc.vector.tensor_tensor(clip_first[:, t, :], t0[:, t, :], high_first[:, t, :], ALU.min)
             scale_clip(t, slice(0, S), clip_first[:, t, :])
             add_turned(t, scaled, stop=t == 1)
-        for n in range(S // P):
-            cols = slice(n * P, (n + 1) * P)
+        for n, cols in enumerate(chunks):
             part = slice(n % 2 * P, (n % 2 + 1) * P)
             if n % 2 == 0:
                 for m in range(2):
@@ -265,7 +257,7 @@ def tile_picked_yosqp_relax_p_kernel(tc, x_words, x_scales, w1, dual, low, high,
                 scale_clip(2 + e, cols, clip[:, e, :])
                 if n == 0:
                     add_turned(2 + e, scaled, stop=e == 1)
-            if n in (0, 2):
+            if n % 2 == 0:
                 turn_back(n // 2, "clip%d" % n)
         rr_first = sb.tile([P, P, PACK], BF16, name="rr0", align_bytes=64)
         nc.scalar.copy(
@@ -277,7 +269,7 @@ def tile_picked_yosqp_relax_p_kernel(tc, x_words, x_scales, w1, dual, low, high,
         rr, codes, scales, acc = {0: rr_first}, {}, {}, {}
 
         def residual(q):
-            rr[q] = sb.tile([P, WIDTHS[q], PACK], BF16, name="rr%d" % q, align_bytes=64)
+            rr[q] = sb.tile([P, P, PACK], BF16, name="rr%d" % q, align_bytes=64)
             nc.vector.tensor_tensor(
                 rr[q][:].rearrange("p (c i) t -> p c t i", i=2),
                 scaled[:, :, chunks[q]].rearrange("p t (c i) -> p c t i", i=2),
@@ -286,14 +278,14 @@ def tile_picked_yosqp_relax_p_kernel(tc, x_words, x_scales, w1, dual, low, high,
             )
 
         def quantize(q):
-            codes[q] = sb.tile([P, WIDTHS[q]], U32, name="rr_codes%d" % q, align_bytes=64)
-            scales[q] = sb.tile([P, WIDTHS[q]], U8, name="rr_scales%d" % q, align_bytes=64)
+            codes[q] = sb.tile([P, P], U32, name="rr_codes%d" % q, align_bytes=64)
+            scales[q] = sb.tile([P, P], U8, name="rr_scales%d" % q, align_bytes=64)
             nc.vector.quantize_mx(
                 out=codes[q][:].bitcast(FP8X4), scales=scales[q][:], in_=rr[q][:].rearrange("p j t -> p (j t)")
             )
 
         def product(q):
-            acc[q] = ps.tile([P, OUT_BLOCKS, WIDTHS[q]], F32, name="acc%d" % q, tag="bank%d" % q)
+            acc[q] = ps.tile([P, OUT_BLOCKS, P], F32, name="acc%d" % q, tag="bank%d" % q)
             for h in range(OUT_BLOCKS):
                 nc.tensor.matmul_mx(
                     out=acc[q][:, h, :],
@@ -306,7 +298,7 @@ def tile_picked_yosqp_relax_p_kernel(tc, x_words, x_scales, w1, dual, low, high,
                 )
 
         def finish(q):
-            res = sb.tile([P, OUT_BLOCKS, WIDTHS[q]], F32, name="res%d" % q)
+            res = sb.tile([P, OUT_BLOCKS, P], F32, name="res%d" % q)
             nc.vector.tensor_tensor(res[:], acc[q][:], lin_sb[:, :, chunks[q]], ALU.add)
             nc.sync.dma_start(out=out_blocks[:, :, chunks[q]], in_=res[:])
 
@@ -319,5 +311,10 @@ def tile_picked_yosqp_relax_p_kernel(tc, x_words, x_scales, w1, dual, low, high,
         for q in (0, 3):
             quantize(q)
             product(q)
-        for q in (1, 2, 0, 3):
+        for q in (1, 2, 0):
             finish(q)
+        last = CHUNKS - 1
+        for h in range(OUT_BLOCKS):
+            res = sb.tile([P, P], F32, name="res_last%d" % h)
+            nc.vector.tensor_tensor(res[:], acc[last][:, h, :], lin_sb[:, h, chunks[last]], ALU.add)
+            nc.sync.dma_start(out=out_blocks[:, h, chunks[last]], in_=res[:])

@@ -51,9 +51,9 @@ def tile_picked_yosqp_relax_p_kernel(tc, x_words, x_scales, w1, dual, low, high,
 
         nc.vector.memset(table_scales[:].bitcast(I32), 0)
 
-        def load_w1(g):
-            rows = w1[g * K_PASS : (g + 1) * K_PASS, :]
-            nc.sync.dma_start(out=w1_raw[g][:], in_=rows.rearrange("(p j) c -> p j c", j=PACK))
+        def load_w1(g, part):
+            rows = w1[g * K_PASS : (g + 1) * K_PASS, :].rearrange("(p j) c -> p j c", j=PACK)
+            nc.sync.dma_start(out=w1_raw[g][:, part, :], in_=rows[:, part, :])
 
         def load_scales(rows):
             for q in rows:
@@ -69,12 +69,13 @@ def tile_picked_yosqp_relax_p_kernel(tc, x_words, x_scales, w1, dual, low, high,
         def planes_of(src):
             return src.rearrange("(p t) j -> p t j", t=PACK)
 
-        load_w1(0)
+        load_w1(0, slice(0, 2))
         nc.sync.dma_start(offsets[:], offs)
         load_scales((0, 1))
+        load_w1(0, slice(2, PACK))
         load_words(0)
         load_scales((2, 3))
-        load_w1(1)
+        load_w1(1, slice(0, PACK))
         load_words(1)
         dual_planes = planes_of(dual)
         nc.sync.dma_start(out=dual_first[0][:], in_=dual_planes[:, 0, :])

@@ -51,9 +51,9 @@ def tile_picked_yosqp_relax_p_kernel(tc, x_words, x_scales, w1, dual, low, high,
 
         nc.vector.memset(table_scales[:].bitcast(I32), 0)
 
-        def load_w1(g, part):
-            rows = w1[g * K_PASS : (g + 1) * K_PASS, :].rearrange("(p j) c -> p j c", j=PACK)
-            nc.sync.dma_start(out=w1_raw[g][:, part, :], in_=rows[:, part, :])
+        def load_w1(g):
+            rows = w1[g * K_PASS : (g + 1) * K_PASS, :]
+            nc.sync.dma_start(out=w1_raw[g][:], in_=rows.rearrange("(p j) c -> p j c", j=PACK))
 
         def load_scales(rows):
             for q in rows:
@@ -63,20 +63,21 @@ def tile_picked_yosqp_relax_p_kernel(tc, x_words, x_scales, w1, dual, low, high,
                         in_=x_scales[g, q : 4 * QUADRANTS : 4, :].bitcast(I32),
                     )
 
-        def load_words(g):
-            nc.sync.dma_start(out=table[g][:].bitcast(I32), in_=x_words[g].rearrange("p n t -> p (n t)").bitcast(I32))
+        def load_words(g, cols):
+            words = x_words[g].rearrange("p n t -> p (n t)").bitcast(I32)
+            nc.sync.dma_start(out=table[g][:, cols].bitcast(I32), in_=words[:, cols])
 
         def planes_of(src):
             return src.rearrange("(p t) j -> p t j", t=PACK)
 
-        load_w1(0, slice(0, 2))
+        load_words(0, slice(0, T // 2))
         nc.sync.dma_start(offsets[:], offs)
         load_scales((0, 1))
-        load_w1(0, slice(2, PACK))
-        load_words(0)
+        load_words(0, slice(T // 2, T))
+        load_w1(0)
         load_scales((2, 3))
-        load_w1(1, slice(0, PACK))
-        load_words(1)
+        load_w1(1)
+        load_words(1, slice(0, T))
         dual_planes = planes_of(dual)
         nc.sync.dma_start(out=dual_first[0][:], in_=dual_planes[:, 0, :])
         nc.sync.dma_start(out=dual_second[:], in_=dual_planes[:, 2:PACK, :])
@@ -120,10 +121,9 @@ def tile_picked_yosqp_relax_p_kernel(tc, x_words, x_scales, w1, dual, low, high,
             return codes, scales
 
         w1_codes0, w1_scales0 = quantize_w1(0)
-        x0, x_sc = [], []
-        for u in range(2):
-            x0.append(gather_half("x0", U32, table[0], u))
-            x_sc.append(gather_half("x_sc", U8, table_scales, u))
+        x0 = [gather_half("x0", U32, table[0], u) for u in range(2)]
+        x_scales_sb = sb.tile([P, S], U8, name="x_scales_sb", align_bytes=64)
+        nc.vector.tensor_copy(x_scales_sb[:], table_scales[:].indirect(offsets[:]))
         w1_codes1, w1_scales1 = quantize_w1(1)
         x1 = [gather_half("x1", U32, table[1], u) for u in range(2)]
 
@@ -137,7 +137,7 @@ def tile_picked_yosqp_relax_p_kernel(tc, x_words, x_scales, w1, dual, low, high,
                     lhsT=w1_codes0[:, t * P : (t + 1) * P].bitcast(FP8X4),
                     lhsT_scale=w1_scales0[:, t * P : (t + 1) * P],
                     rhs=x0[u][:].bitcast(FP8X4),
-                    rhs_scale=x_sc[u][:],
+                    rhs_scale=x_scales_sb[:, halves[u]],
                     start=True,
                     stop=False,
                 )
@@ -148,7 +148,7 @@ def tile_picked_yosqp_relax_p_kernel(tc, x_words, x_scales, w1, dual, low, high,
                     lhsT=w1_codes1[:, t * P : (t + 1) * P].bitcast(FP8X4),
                     lhsT_scale=w1_scales1[:, t * P : (t + 1) * P],
                     rhs=x1[u][:].bitcast(FP8X4),
-                    rhs_scale=x_sc[u][4:P, :],
+                    rhs_scale=x_scales_sb[4:P, halves[u]],
                     start=False,
                     stop=True,
                 )

@@ -101,9 +101,12 @@ def tile_picked_yosqp_relax_p_kernel(tc, x_words, x_scales, w1, dual, low, high,
         identity = sb.tile([P, P], F32, name="identity")
         make_identity(nc, identity[:])
 
-        def gather_half(name, dtype, window, u):
-            picked = sb.tile([P, HALF], dtype, name="%s_%d" % (name, u), align_bytes=64)
-            nc.vector.tensor_copy(picked[:], window[:].indirect(offsets[:, LIST_COLS * u : LIST_COLS * (u + 1)]))
+        halves = [slice(u * HALF, (u + 1) * HALF) for u in range(2)]
+        def gather_words(g):
+            picked = sb.tile([P, S], U32, name="x%d" % g, align_bytes=64)
+            for u in range(2):
+                entries = offsets[:, LIST_COLS * u : LIST_COLS * (u + 1)]
+                nc.vector.tensor_copy(picked[:, halves[u]], table[g][:].indirect(entries))
             return picked
 
         def quantize_w1(g):
@@ -121,36 +124,26 @@ def tile_picked_yosqp_relax_p_kernel(tc, x_words, x_scales, w1, dual, low, high,
             return codes, scales
 
         w1_codes0, w1_scales0 = quantize_w1(0)
-        x0 = [gather_half("x0", U32, table[0], u) for u in range(2)]
+        x0 = gather_words(0)
         x_scales_sb = sb.tile([P, S], U8, name="x_scales_sb", align_bytes=64)
         nc.vector.tensor_copy(x_scales_sb[:], table_scales[:].indirect(offsets[:]))
         w1_codes1, w1_scales1 = quantize_w1(1)
-        x1 = [gather_half("x1", U32, table[1], u) for u in range(2)]
+        x1 = gather_words(1)
 
-        halves = [slice(u * HALF, (u + 1) * HALF) for u in range(2)]
+        groups = [(u, t, halves[u]) for u in range(2) for t in (0, 2, 3)] + [(0, 1, slice(0, S))]
         y = {}
-        for u in range(2):
-            for t in range(PACK):
-                y[u, t] = ps.tile([P, HALF], F32, name="y%d%d" % (u, t), tag="bank%d" % (PACK * u + t))
+        for u, t, cols in groups:
+            y[u, t] = ps.tile([P, cols.stop - cols.start], F32, name="y%d%d" % (u, t), tag="bank%d" % (PACK * u + t))
+        for g, (x, codes_g, scales_g) in enumerate(((x0, w1_codes0, w1_scales0), (x1, w1_codes1, w1_scales1))):
+            for u, t, cols in groups:
                 nc.tensor.matmul_mx(
                     out=y[u, t][:],
-                    lhsT=w1_codes0[:, t * P : (t + 1) * P].bitcast(FP8X4),
-                    lhsT_scale=w1_scales0[:, t * P : (t + 1) * P],
-                    rhs=x0[u][:].bitcast(FP8X4),
-                    rhs_scale=x_scales_sb[:, halves[u]],
-                    start=True,
-                    stop=False,
-                )
-        for u in range(2):
-            for t in (0, 2, 3, 1):
-                nc.tensor.matmul_mx(
-                    out=y[u, t][:],
-                    lhsT=w1_codes1[:, t * P : (t + 1) * P].bitcast(FP8X4),
-                    lhsT_scale=w1_scales1[:, t * P : (t + 1) * P],
-                    rhs=x1[u][:].bitcast(FP8X4),
-                    rhs_scale=x_scales_sb[4:P, halves[u]],
-                    start=False,
-                    stop=True,
+                    lhsT=codes_g[:, t * P : (t + 1) * P].bitcast(FP8X4),
+                    lhsT_scale=scales_g[:, t * P : (t + 1) * P],
+                    rhs=x[:, cols].bitcast(FP8X4),
+                    rhs_scale=x_scales_sb[4 * g : P, cols],
+                    start=g == 0,
+                    stop=g == PASSES - 1,
                 )
 
         t0 = sb.tile([P, PACK, S], F32, name="t0")
@@ -181,7 +174,8 @@ def tile_picked_yosqp_relax_p_kernel(tc, x_words, x_scales, w1, dual, low, high,
         for u in range(2):
             for t in range(2, PACK):
                 make_t0(u, t)
-        first_plane(1)
+        nc.vector.scalar_tensor_tensor(t0[:, 1, :], dual_plane[1], 0.5, y[0, 1][:], ALU.mult, ALU.add)
+        nc.vector.scalar_tensor_tensor(total[:, 1, P:S], y[0, 1][:, P:S], 1.7, dual_plane[1][:, P:S], ALU.mult, ALU.add)
         w2_grouped = []
 
         def round_w2(h):

@@ -24,7 +24,7 @@ QUADRANTS = P // 32
 HALF = S // 2
 LIST_COLS = HALF // 16
 OUT_BLOCKS = N // P
-SCALAR_M = (48, 64)
+SCALAR_M = (48, 44)
 CHUNKS = S // P
 
 
@@ -44,7 +44,7 @@ def tile_picked_yosqp_relax_p_kernel(tc, x_words, x_scales, w1, dual, low, high,
         dual_plane = [dual_first[0][:], dual_first[1][:], dual_second[:, 0, :], dual_second[:, 1, :]]
         low_first = [sb.tile([P, S], F32, name="low_first%d" % t, tag="low_first%d" % t, align_bytes=64) for t in range(2)]
         high_first = sb.tile([P, 2, S], F32, name="high_first")
-        low_second = [sb.tile([P, 2, HALF], F32, name="low_second%d" % u, tag="low_second%d" % u, align_bytes=64) for u in range(2)]
+        low_second = [sb.tile([P, 2, HALF], F32, name="low_second%d" % u, align_bytes=64) for u in range(2)]
         high_second = [sb.tile([P, 2, HALF], F32, name="high_second%d" % u) for u in range(2)]
         w2_raw = sb.tile([P, PACK, N], F32, name="w2_raw", tag="w2_raw")
         lin_sb = sb.tile([P, OUT_BLOCKS, S], F32, name="lin_sb")
@@ -102,6 +102,7 @@ def tile_picked_yosqp_relax_p_kernel(tc, x_words, x_scales, w1, dual, low, high,
         make_identity(nc, identity[:])
 
         halves = [slice(u * HALF, (u + 1) * HALF) for u in range(2)]
+
         def gather_words(g):
             picked = sb.tile([P, S], U32, name="x%d" % g, align_bytes=64)
             for u in range(2):
@@ -134,12 +135,13 @@ def tile_picked_yosqp_relax_p_kernel(tc, x_words, x_scales, w1, dual, low, high,
         y = {}
         for u, t, cols in groups:
             y[u, t] = ps.tile([P, cols.stop - cols.start], F32, name="y%d%d" % (u, t), tag="bank%d" % (PACK * u + t))
-        for g, (x, codes_g, scales_g) in enumerate(((x0, w1_codes0, w1_scales0), (x1, w1_codes1, w1_scales1))):
+        operands = ((x0, w1_codes0, w1_scales0), (x1, w1_codes1, w1_scales1))
+        for g, (x, w1_codes, w1_scales) in enumerate(operands):
             for u, t, cols in groups:
                 nc.tensor.matmul_mx(
                     out=y[u, t][:],
-                    lhsT=codes_g[:, t * P : (t + 1) * P].bitcast(FP8X4),
-                    lhsT_scale=scales_g[:, t * P : (t + 1) * P],
+                    lhsT=w1_codes[:, t * P : (t + 1) * P].bitcast(FP8X4),
+                    lhsT_scale=w1_scales[:, t * P : (t + 1) * P],
                     rhs=x[:, cols].bitcast(FP8X4),
                     rhs_scale=x_scales_sb[4 * g : P, cols],
                     start=g == 0,
@@ -148,34 +150,29 @@ def tile_picked_yosqp_relax_p_kernel(tc, x_words, x_scales, w1, dual, low, high,
 
         t0 = sb.tile([P, PACK, S], F32, name="t0")
 
-        def make_t0(u, t):
-            nc.vector.scalar_tensor_tensor(
-                t0[:, t, halves[u]], dual_plane[t][:, halves[u]], 0.5, y[u, t][:], ALU.mult, ALU.add
-            )
+        def make_t0(t, cols, y_part):
+            nc.vector.scalar_tensor_tensor(t0[:, t, cols], dual_plane[t][:, cols], 0.5, y_part, ALU.mult, ALU.add)
 
         total = sb.tile([P, PACK, S], F32, name="total")
         for e in range(2):
             nc.scalar.activation(total[:, 2 + e, halves[0]], y[0, 2 + e][:], COPY, scale=1.7)
         nc.gpsimd.tensor_tensor(total[:, 2:PACK, P:HALF], total[:, 2:PACK, P:HALF], dual_second[:, :, P:HALF], ALU.add)
-        y_term = sb.tile([P, 2, HALF], F32, name="y_term", tag="y_term", align_bytes=64)
+        y_term = sb.tile([P, 2, HALF], F32, name="y_term", align_bytes=64)
         for e in range(2):
             nc.scalar.activation(y_term[:, e, :], y[1, 2 + e][:], COPY, scale=1.7)
         nc.gpsimd.tensor_tensor(total[:, 2:PACK, halves[1]], y_term[:], dual_second[:, :, halves[1]], ALU.add)
 
-        def first_plane(t):
-            for u, skip in enumerate((P, 0)):
-                make_t0(u, t)
-                cols = slice(u * HALF + skip, (u + 1) * HALF)
-                nc.vector.scalar_tensor_tensor(
-                    total[:, t, cols], y[u, t][:, skip:HALF], 1.7, dual_plane[t][:, cols], ALU.mult, ALU.add
-                )
+        def make_total(t, cols, y_part):
+            nc.vector.scalar_tensor_tensor(total[:, t, cols], y_part, 1.7, dual_plane[t][:, cols], ALU.mult, ALU.add)
 
-        first_plane(0)
+        for u, skip in enumerate((P, 0)):
+            make_t0(0, halves[u], y[u, 0][:])
+            make_total(0, slice(u * HALF + skip, (u + 1) * HALF), y[u, 0][:, skip:HALF])
         for u in range(2):
             for t in range(2, PACK):
-                make_t0(u, t)
-        nc.vector.scalar_tensor_tensor(t0[:, 1, :], dual_plane[1], 0.5, y[0, 1][:], ALU.mult, ALU.add)
-        nc.vector.scalar_tensor_tensor(total[:, 1, P:S], y[0, 1][:, P:S], 1.7, dual_plane[1][:, P:S], ALU.mult, ALU.add)
+                make_t0(t, halves[u], y[u, t][:])
+        make_t0(1, slice(0, S), y[0, 1][:])
+        make_total(1, slice(P, S), y[0, 1][:, P:S])
         w2_grouped = []
 
         def round_w2(h):

@@ -26,6 +26,7 @@ LIST_COLS = HALF // 16
 OUT_BLOCKS = N // P
 SCALAR_M = (48, 44)
 CHUNKS = S // P
+ROW = 256
 
 
 def tile_picked_yosqp_relax_p_kernel(tc, x_words, x_scales, w1, dual, low, high, rho, w2, lin, offs, out):
@@ -34,20 +35,20 @@ def tile_picked_yosqp_relax_p_kernel(tc, x_words, x_scales, w1, dual, low, high,
         sb = ctx.enter_context(tc.tile_pool(name="sb", bufs=1))
         ps = ctx.enter_context(tc.psum_pool(name="ps", bufs=1))
 
-        w1_raw = [sb.tile([P, PACK, H], F32, name="w1_raw%d" % g) for g in range(PASSES)]
-        table = [sb.tile([P, T], U32, name="table%d" % g) for g in range(PASSES)]
-        table_scales = sb.tile([P, T], U8, name="table_scales")
+        w1_raw = [sb.tile([P, PACK, H], F32, name="w1_raw%d" % g, align_bytes=ROW) for g in range(PASSES)]
+        table = [sb.tile([P, T], U32, name="table%d" % g, align_bytes=ROW) for g in range(PASSES)]
+        table_scales = sb.tile([P, T], U8, name="table_scales", align_bytes=ROW)
         offsets = sb.tile([P, S // 16], U16, name="offsets")
         rho_sb = sb.tile([P, PACK], F32, name="rho_sb")
-        dual_first = [sb.tile([P, S], F32, name="dual%d" % t) for t in range(2)]
-        dual_second = sb.tile([P, 2, S], F32, name="dual_second")
+        dual_first = [sb.tile([P, S], F32, name="dual%d" % t, align_bytes=ROW) for t in range(2)]
+        dual_second = sb.tile([P, 2, S], F32, name="dual_second", align_bytes=ROW)
         dual_plane = [dual_first[0][:], dual_first[1][:], dual_second[:, 0, :], dual_second[:, 1, :]]
-        low_first = [sb.tile([P, S], F32, name="low_first%d" % t, tag="low_first%d" % t, align_bytes=64) for t in range(2)]
-        high_first = sb.tile([P, 2, S], F32, name="high_first")
-        low_second = [sb.tile([P, 2, HALF], F32, name="low_second%d" % u, align_bytes=64) for u in range(2)]
-        high_second = [sb.tile([P, 2, HALF], F32, name="high_second%d" % u) for u in range(2)]
-        w2_raw = sb.tile([P, PACK, N], F32, name="w2_raw", tag="w2_raw")
-        lin_sb = sb.tile([P, OUT_BLOCKS, S], F32, name="lin_sb")
+        low_first = [sb.tile([P, S], F32, name="low_first%d" % t, tag="low_first%d" % t, align_bytes=ROW) for t in range(2)]
+        high_first = sb.tile([P, 2, S], F32, name="high_first", align_bytes=ROW)
+        low_second = [sb.tile([P, 2, HALF], F32, name="low_second%d" % u, align_bytes=ROW) for u in range(2)]
+        high_second = [sb.tile([P, 2, HALF], F32, name="high_second%d" % u, align_bytes=ROW) for u in range(2)]
+        w2_raw = sb.tile([P, PACK, N], F32, name="w2_raw", tag="w2_raw", align_bytes=ROW)
+        lin_sb = sb.tile([P, OUT_BLOCKS, S], F32, name="lin_sb", align_bytes=ROW)
 
         nc.vector.memset(table_scales[:].bitcast(I32), 0)
 
@@ -204,7 +205,7 @@ def tile_picked_yosqp_relax_p_kernel(tc, x_words, x_scales, w1, dual, low, high,
 
         for h in range(OUT_BLOCKS):
             round_w2(h)
-        linear = sb.tile([P, PACK, S], F32, name="linear", tag="w2_raw")
+        linear = sb.tile([P, PACK, S], F32, name="linear", tag="w2_raw", align_bytes=ROW)
         dual_term = sb.tile([P, PACK, P], F32, name="dual_term")
         for t in (0, 2, 3, 1):
             nc.scalar.activation(dual_term[:, t, :], dual_plane[t][:, 0:P], COPY, scale=rho_neg[:, t : t + 1])
@@ -227,7 +228,7 @@ def tile_picked_yosqp_relax_p_kernel(tc, x_words, x_scales, w1, dual, low, high,
 
         for t in range(2):
             nc.vector.tensor_tensor(t0[:, t, :], t0[:, t, :], low_first[t][:], ALU.max)
-        w2_codes = sb.tile([P, N], U32, name="w2_codes", tag="low_first0", align_bytes=64)
+        w2_codes = sb.tile([P, N], U32, name="w2_codes", tag="low_first0", align_bytes=ROW)
         for h in range(OUT_BLOCKS):
             quantize_w2(h)
         clip_first = sb.tile([P, 2, S], F32, name="clip_first")
@@ -290,7 +291,7 @@ def tile_picked_yosqp_relax_p_kernel(tc, x_words, x_scales, w1, dual, low, high,
                 )
 
         def finish(q):
-            res = sb.tile([P, OUT_BLOCKS, P], F32, name="res%d" % q)
+            res = sb.tile([P, OUT_BLOCKS, P], F32, name="res%d" % q, align_bytes=ROW)
             nc.vector.tensor_tensor(res[:], acc[q][:], lin_sb[:, :, chunks[q]], ALU.add)
             nc.sync.dma_start(out=out_blocks[:, :, chunks[q]], in_=res[:])
 
@@ -307,6 +308,6 @@ def tile_picked_yosqp_relax_p_kernel(tc, x_words, x_scales, w1, dual, low, high,
             finish(q)
         last = CHUNKS - 1
         for h in range(OUT_BLOCKS):
-            res = sb.tile([P, P], F32, name="res_last%d" % h)
+            res = sb.tile([P, P], F32, name="res_last%d" % h, align_bytes=ROW)
             nc.vector.tensor_tensor(res[:], acc[last][:, h, :], lin_sb[:, h, chunks[last]], ALU.add)
             nc.sync.dma_start(out=out_blocks[:, h, chunks[last]], in_=res[:])

@@ -99,27 +99,27 @@ def tile_picked_yosqp_relax_p_kernel(tc, x_words, x_scales, w1, dual, low, high,
         nc.scalar.activation(rho_neg[:], rho_sb[:], COPY, scale=-1.0)
         rho_y = sb.tile([P, PACK], F32, name="rho_y")
         nc.scalar.activation(rho_y[:], rho_sb[:], COPY, scale=-1.7)
-        identity = sb.tile([P, P], F32, name="identity")
+        identity = sb.tile([P, P], F32, name="identity", align_bytes=ROW)
         make_identity(nc, identity[:])
 
         halves = [slice(u * HALF, (u + 1) * HALF) for u in range(2)]
 
         def gather_words(g):
-            picked = sb.tile([P, S], U32, name="x%d" % g, align_bytes=64)
+            picked = sb.tile([P, S], U32, name="x%d" % g, align_bytes=ROW)
             for u in range(2):
                 entries = offsets[:, LIST_COLS * u : LIST_COLS * (u + 1)]
                 nc.vector.tensor_copy(picked[:, halves[u]], table[g][:].indirect(entries))
             return picked
 
         def quantize_w1(g):
-            grouped = sb.tile([P, PACK, P, PACK], BF16, name="w1_grouped%d" % g, align_bytes=64)
+            grouped = sb.tile([P, PACK, P, PACK], BF16, name="w1_grouped%d" % g, align_bytes=ROW)
             dst = grouped[:].rearrange("p (a e) m j -> p a m j e", e=2)
             src = w1_raw[g][:].rearrange("p j (m a e) -> p a m j e", a=2, e=2)
             share = SCALAR_M[g]
             nc.scalar.copy(dst[:, :, 0:share], src[:, :, 0:share])
             nc.vector.tensor_copy(dst[:, :, share:P], src[:, :, share:P])
-            codes = sb.tile([P, H], U32, name="w1_codes%d" % g, align_bytes=64)
-            scales = sb.tile([P, H], U8, name="w1_scales%d" % g, align_bytes=64)
+            codes = sb.tile([P, H], U32, name="w1_codes%d" % g, align_bytes=ROW)
+            scales = sb.tile([P, H], U8, name="w1_scales%d" % g, align_bytes=ROW)
             nc.vector.quantize_mx(
                 out=codes[:].bitcast(FP8X4), scales=scales[:], in_=grouped[:].rearrange("p t m j -> p (t m j)")
             )
@@ -127,7 +127,7 @@ def tile_picked_yosqp_relax_p_kernel(tc, x_words, x_scales, w1, dual, low, high,
 
         w1_codes0, w1_scales0 = quantize_w1(0)
         x0 = gather_words(0)
-        x_scales_sb = sb.tile([P, S], U8, name="x_scales_sb", align_bytes=64)
+        x_scales_sb = sb.tile([P, S], U8, name="x_scales_sb", align_bytes=ROW)
         nc.vector.tensor_copy(x_scales_sb[:], table_scales[:].indirect(offsets[:]))
         w1_codes1, w1_scales1 = quantize_w1(1)
         x1 = gather_words(1)
@@ -149,16 +149,16 @@ def tile_picked_yosqp_relax_p_kernel(tc, x_words, x_scales, w1, dual, low, high,
                     stop=g == PASSES - 1,
                 )
 
-        t0 = sb.tile([P, PACK, S], F32, name="t0")
+        t0 = sb.tile([P, PACK, S], F32, name="t0", align_bytes=ROW)
 
         def make_t0(t, cols, y_part):
             nc.vector.scalar_tensor_tensor(t0[:, t, cols], dual_plane[t][:, cols], 0.5, y_part, ALU.mult, ALU.add)
 
-        total = sb.tile([P, PACK, S], F32, name="total")
+        total = sb.tile([P, PACK, S], F32, name="total", align_bytes=ROW)
         for e in range(2):
             nc.scalar.activation(total[:, 2 + e, halves[0]], y[0, 2 + e][:], COPY, scale=1.7)
         nc.gpsimd.tensor_tensor(total[:, 2:PACK, P:HALF], total[:, 2:PACK, P:HALF], dual_second[:, :, P:HALF], ALU.add)
-        y_term = sb.tile([P, 2, HALF], F32, name="y_term", align_bytes=64)
+        y_term = sb.tile([P, 2, HALF], F32, name="y_term", align_bytes=ROW)
         for e in range(2):
             nc.scalar.activation(y_term[:, e, :], y[1, 2 + e][:], COPY, scale=1.7)
         nc.gpsimd.tensor_tensor(total[:, 2:PACK, halves[1]], y_term[:], dual_second[:, :, halves[1]], ALU.add)
@@ -177,7 +177,7 @@ def tile_picked_yosqp_relax_p_kernel(tc, x_words, x_scales, w1, dual, low, high,
         w2_grouped = []
 
         def round_w2(h):
-            grouped = sb.tile([P, P, PACK], BF16, name="w2_grouped%d" % h, align_bytes=64)
+            grouped = sb.tile([P, P, PACK], BF16, name="w2_grouped%d" % h, align_bytes=ROW)
             nc.scalar.copy(
                 grouped[:].rearrange("p (c i) j -> p c j i", i=4),
                 w2_raw[:, :, h * P : (h + 1) * P].rearrange("p j (c i) -> p c j i", i=4),
@@ -190,11 +190,11 @@ def tile_picked_yosqp_relax_p_kernel(tc, x_words, x_scales, w1, dual, low, high,
             )
 
         def turn_back(a, tag):
-            pairs = sb.tile([P, P, 2], BF16, name="pairs%d" % a, tag=tag)
+            pairs = sb.tile([P, P, 2], BF16, name="pairs%d" % a, tag=tag, align_bytes=ROW)
             nc.scalar.copy(pairs[:], turned[a][:].rearrange("j e p -> j p e"))
             nc.tensor.transpose(back[:, a, :], pairs[:].rearrange("j p e -> j (p e)").bitcast(F32), identity[:])
 
-        w2_scales = sb.tile([P, N], U8, name="w2_scales", align_bytes=64)
+        w2_scales = sb.tile([P, N], U8, name="w2_scales", align_bytes=ROW)
 
         def quantize_w2(h):
             nc.vector.quantize_mx(
@@ -206,7 +206,7 @@ def tile_picked_yosqp_relax_p_kernel(tc, x_words, x_scales, w1, dual, low, high,
         for h in range(OUT_BLOCKS):
             round_w2(h)
         linear = sb.tile([P, PACK, S], F32, name="linear", tag="w2_raw", align_bytes=ROW)
-        dual_term = sb.tile([P, PACK, P], F32, name="dual_term")
+        dual_term = sb.tile([P, PACK, P], F32, name="dual_term", align_bytes=ROW)
         for t in (0, 2, 3, 1):
             nc.scalar.activation(dual_term[:, t, :], dual_plane[t][:, 0:P], COPY, scale=rho_neg[:, t : t + 1])
             if t < 2:
@@ -221,7 +221,7 @@ def tile_picked_yosqp_relax_p_kernel(tc, x_words, x_scales, w1, dual, low, high,
             add_turned(t, linear)
 
         chunks = [slice(q * P, (q + 1) * P) for q in range(CHUNKS)]
-        scaled = sb.tile([P, PACK, S], F32, name="scaled")
+        scaled = sb.tile([P, PACK, S], F32, name="scaled", align_bytes=ROW)
 
         def scale_clip(t, cols, clip):
             nc.scalar.activation(scaled[:, t, cols], clip, COPY, scale=rho_clip[:, t : t + 1])
@@ -231,7 +231,7 @@ def tile_picked_yosqp_relax_p_kernel(tc, x_words, x_scales, w1, dual, low, high,
         w2_codes = sb.tile([P, N], U32, name="w2_codes", tag="low_first0", align_bytes=ROW)
         for h in range(OUT_BLOCKS):
             quantize_w2(h)
-        clip_first = sb.tile([P, 2, S], F32, name="clip_first")
+        clip_first = sb.tile([P, 2, S], F32, name="clip_first", align_bytes=ROW)
         for t in range(2):
             nc.vector.tensor_tensor(clip_first[:, t, :], t0[:, t, :], high_first[:, t, :], ALU.min)
             scale_clip(t, slice(0, S), clip_first[:, t, :])
@@ -244,7 +244,7 @@ def tile_picked_yosqp_relax_p_kernel(tc, x_words, x_scales, w1, dual, low, high,
                     nc.vector.tensor_tensor(
                         t0[:, 2:PACK, both], t0[:, 2:PACK, both], low_second[n // 2][:, :, m * P : (m + 1) * P], ALU.max
                     )
-            clip = sb.tile([P, 2, P], F32, name="clip%d" % n, tag="clip%d" % n)
+            clip = sb.tile([P, 2, P], F32, name="clip%d" % n, tag="clip%d" % n, align_bytes=ROW)
             nc.vector.tensor_tensor(clip[:], t0[:, 2:PACK, cols], high_second[n // 2][:, :, part], ALU.min)
             for e in range(2):
                 scale_clip(2 + e, cols, clip[:, e, :])
@@ -252,7 +252,7 @@ def tile_picked_yosqp_relax_p_kernel(tc, x_words, x_scales, w1, dual, low, high,
                     add_turned(2 + e, scaled, stop=e == 1)
             if n % 2 == 0:
                 turn_back(n // 2, "clip%d" % n)
-        rr_first = sb.tile([P, P, PACK], BF16, name="rr0", align_bytes=64)
+        rr_first = sb.tile([P, P, PACK], BF16, name="rr0", align_bytes=ROW)
         nc.scalar.copy(
             rr_first[:].rearrange("p j t -> p (j t)").bitcast(F32).rearrange("p (j a) -> p j a", a=2),
             back[:].rearrange("p a j -> p j a"),
@@ -262,7 +262,7 @@ def tile_picked_yosqp_relax_p_kernel(tc, x_words, x_scales, w1, dual, low, high,
         rr, codes, scales, acc = {0: rr_first}, {}, {}, {}
 
         def residual(q):
-            rr[q] = sb.tile([P, P, PACK], BF16, name="rr%d" % q, align_bytes=64)
+            rr[q] = sb.tile([P, P, PACK], BF16, name="rr%d" % q, align_bytes=ROW)
             nc.vector.tensor_tensor(
                 rr[q][:].rearrange("p (c i) t -> p c t i", i=2),
                 scaled[:, :, chunks[q]].rearrange("p t (c i) -> p c t i", i=2),
@@ -271,8 +271,8 @@ def tile_picked_yosqp_relax_p_kernel(tc, x_words, x_scales, w1, dual, low, high,
             )
 
         def quantize(q):
-            codes[q] = sb.tile([P, P], U32, name="rr_codes%d" % q, align_bytes=64)
-            scales[q] = sb.tile([P, P], U8, name="rr_scales%d" % q, align_bytes=64)
+            codes[q] = sb.tile([P, P], U32, name="rr_codes%d" % q, align_bytes=ROW)
+            scales[q] = sb.tile([P, P], U8, name="rr_scales%d" % q, align_bytes=ROW)
             nc.vector.quantize_mx(
                 out=codes[q][:].bitcast(FP8X4), scales=scales[q][:], in_=rr[q][:].rearrange("p j t -> p (j t)")
             )

from contextlib import ExitStack

import concourse.mybir as mybir
from concourse.masks import make_identity

K, T, S, H, N = 1024, 2048, 512, 512, 256
FLOPS = 2 * K * H * S + 2 * H * N * S

F32 = mybir.dt.float32
BF16 = mybir.dt.bfloat16
I32 = mybir.dt.int32
U32 = mybir.dt.uint32
U16 = mybir.dt.uint16
U8 = mybir.dt.uint8
FP8X4 = mybir.dt.float8_e4m3fn_x4
ALU = mybir.AluOpType
COPY = mybir.ActivationFunctionType.Copy

P = 128
PACK = 4
K_PASS = P * PACK
PASSES = K // K_PASS
QUADRANTS = P // 32
HALF = S // 2
LIST_COLS = HALF // 16
OUT_BLOCKS = N // P
SCALAR_M = (48, 44)
CHUNKS = S // P
ROW = 256


def tile_picked_yosqp_relax_p_kernel(tc, x_words, x_scales, w1, dual, low, high, rho, w2, lin, offs, out):
    nc = tc.nc
    with ExitStack() as ctx:
        sb = ctx.enter_context(tc.tile_pool(name="sb", bufs=1))
        ps = ctx.enter_context(tc.psum_pool(name="ps", bufs=1))

        w1_raw = [sb.tile([P, PACK, H], F32, name="w1_raw%d" % g, align_bytes=ROW) for g in range(PASSES)]
        table = [sb.tile([P, T], U32, name="table%d" % g, align_bytes=ROW) for g in range(PASSES)]
        table_scales = sb.tile([P, T], U8, name="table_scales", align_bytes=ROW)
        offsets = sb.tile([P, S // 16], U16, name="offsets")
        rho_sb = sb.tile([P, PACK], F32, name="rho_sb")
        dual_first = [sb.tile([P, S], F32, name="dual%d" % t, align_bytes=ROW) for t in range(2)]
        dual_second = sb.tile([P, 2, S], F32, name="dual_second", align_bytes=ROW)
        dual_plane = [dual_first[0][:], dual_first[1][:], dual_second[:, 0, :], dual_second[:, 1, :]]
        low_first = [sb.tile([P, S], F32, name="low_first%d" % t, tag="low_first%d" % t, align_bytes=ROW) for t in range(2)]
        high_first = sb.tile([P, 2, S], F32, name="high_first", align_bytes=ROW)
        low_second = [sb.tile([P, 2, HALF], F32, name="low_second%d" % u, align_bytes=ROW) for u in range(2)]
        high_second = [sb.tile([P, 2, HALF], F32, name="high_second%d" % u, align_bytes=ROW) for u in range(2)]
        w2_raw = sb.tile([P, PACK, N], F32, name="w2_raw", tag="w2_raw", align_bytes=ROW)
        lin_sb = sb.tile([P, OUT_BLOCKS, S], F32, name="lin_sb", align_bytes=ROW)

        nc.vector.memset(table_scales[:].bitcast(I32), 0)

        def load_w1(g):
            rows = w1[g * K_PASS : (g + 1) * K_PASS, :]
            nc.sync.dma_start(out=w1_raw[g][:], in_=rows.rearrange("(p j) c -> p j c", j=PACK))

        def load_scales(rows):
            for q in rows:
                for g in range(PASSES):
                    nc.sync.dma_start(
                        out=table_scales[4 * g + q : P : 32, :].bitcast(I32),
                        in_=x_scales[g, q : 4 * QUADRANTS : 4, :].bitcast(I32),
                    )

        def load_words(g, cols):
            words = x_words[g].rearrange("p n t -> p (n t)").bitcast(I32)
            nc.sync.dma_start(out=table[g][:, cols].bitcast(I32), in_=words[:, cols])

        def planes_of(src):
            return src.rearrange("(p t) j -> p t j", t=PACK)

        load_words(0, slice(0, T // 2))
        nc.sync.dma_start(offsets[:], offs)
        load_scales((0, 1))
        load_words(0, slice(T // 2, T))
        load_w1(0)
        load_scales((2, 3))
        load_w1(1)
        load_words(1, slice(0, T))
        dual_planes = planes_of(dual)
        nc.sync.dma_start(out=dual_first[0][:], in_=dual_planes[:, 0, :])
        nc.sync.dma_start(out=dual_second[:], in_=dual_planes[:, 2:PACK, :])
        nc.sync.dma_start(out=rho_sb[:], in_=rho.rearrange("(p t) o -> p (t o)", t=PACK))
        nc.sync.dma_start(out=w2_raw[:], in_=w2.rearrange("(p j) c -> p j c", j=PACK))
        nc.sync.dma_start(out=dual_first[1][:], in_=dual_planes[:, 1, :])
        for t in range(2):
            nc.sync.dma_start(out=low_first[t][:], in_=planes_of(low)[:, t, :])
        nc.sync.dma_start(out=high_first[:], in_=planes_of(high)[:, 0:2, :])
        for u in range(2):
            for tiles, src in ((low_second, low), (high_second, high)):
                nc.sync.dma_start(out=tiles[u][:], in_=planes_of(src)[:, 2:PACK, u * HALF : (u + 1) * HALF])
        nc.sync.dma_start(out=lin_sb[:], in_=lin.rearrange("(h p) j -> p h j", p=P))

        rho_clip = sb.tile([P, PACK], F32, name="rho_clip")
        nc.scalar.activation(rho_clip[:], rho_sb[:], COPY, scale=3.0)
        rho_neg = sb.tile([P, PACK], F32, name="rho_neg")
        nc.scalar.activation(rho_neg[:], rho_sb[:], COPY, scale=-1.0)
        rho_y = sb.tile([P, PACK], F32, name="rho_y")
        nc.scalar.activation(rho_y[:], rho_sb[:], COPY, scale=-1.7)
        identity = sb.tile([P, P], F32, name="identity", align_bytes=ROW)
        make_identity(nc, identity[:])

        halves = [slice(u * HALF, (u + 1) * HALF) for u in range(2)]

        def gather_words(g):
            picked = sb.tile([P, S], U32, name="x%d" % g, align_bytes=ROW)
            for u in range(2):
                entries = offsets[:, LIST_COLS * u : LIST_COLS * (u + 1)]
                nc.vector.tensor_copy(picked[:, halves[u]], table[g][:].indirect(entries))
            return picked

        def quantize_w1(g):
            grouped = sb.tile([P, PACK, P, PACK], BF16, name="w1_grouped%d" % g, align_bytes=ROW)
            dst = grouped[:].rearrange("p (a e) m j -> p a m j e", e=2)
            src = w1_raw[g][:].rearrange("p j (m a e) -> p a m j e", a=2, e=2)
            share = SCALAR_M[g]
            nc.scalar.copy(dst[:, :, 0:share], src[:, :, 0:share])
            nc.vector.tensor_copy(dst[:, :, share:P], src[:, :, share:P])
            codes = sb.tile([P, H], U32, name="w1_codes%d" % g, align_bytes=ROW)
            scales = sb.tile([P, H], U8, name="w1_scales%d" % g, align_bytes=ROW)
            nc.vector.quantize_mx(
                out=codes[:].bitcast(FP8X4), scales=scales[:], in_=grouped[:].rearrange("p t m j -> p (t m j)")
            )
            return codes, scales

        w1_codes0, w1_scales0 = quantize_w1(0)
        x0 = gather_words(0)
        x_scales_sb = sb.tile([P, S], U8, name="x_scales_sb", align_bytes=ROW)
        nc.vector.tensor_copy(x_scales_sb[:], table_scales[:].indirect(offsets[:]))
        w1_codes1, w1_scales1 = quantize_w1(1)
        x1 = gather_words(1)

        groups = [(u, t, halves[u]) for u in range(2) for t in (0, 2, 3)] + [(0, 1, slice(0, S))]
        y = {}
        for u, t, cols in groups:
            y[u, t] = ps.tile([P, cols.stop - cols.start], F32, name="y%d%d" % (u, t), tag="bank%d" % (PACK * u + t))
        operands = ((x0, w1_codes0, w1_scales0), (x1, w1_codes1, w1_scales1))
        for g, (x, w1_codes, w1_scales) in enumerate(operands):
            for u, t, cols in groups:
                nc.tensor.matmul_mx(
                    out=y[u, t][:],
                    lhsT=w1_codes[:, t * P : (t + 1) * P].bitcast(FP8X4),
                    lhsT_scale=w1_scales[:, t * P : (t + 1) * P],
                    rhs=x[:, cols].bitcast(FP8X4),
                    rhs_scale=x_scales_sb[4 * g : P, cols],
                    start=g == 0,
                    stop=g == PASSES - 1,
                )

        t0 = sb.tile([P, PACK, S], F32, name="t0", align_bytes=ROW)

        def make_t0(t, cols, y_part):
            nc.vector.scalar_tensor_tensor(t0[:, t, cols], dual_plane[t][:, cols], 0.5, y_part, ALU.mult, ALU.add)

        total = sb.tile([P, PACK, S], F32, name="total", align_bytes=ROW)
        for e in range(2):
            nc.scalar.activation(total[:, 2 + e, halves[0]], y[0, 2 + e][:], COPY, scale=1.7)
        nc.gpsimd.tensor_tensor(total[:, 2:PACK, P:HALF], total[:, 2:PACK, P:HALF], dual_second[:, :, P:HALF], ALU.add)
        y_term = sb.tile([P, 2, HALF], F32, name="y_term", align_bytes=ROW)
        for e in range(2):
            nc.scalar.activation(y_term[:, e, :], y[1, 2 + e][:], COPY, scale=1.7)
        nc.gpsimd.tensor_tensor(total[:, 2:PACK, halves[1]], y_term[:], dual_second[:, :, halves[1]], ALU.add)

        def make_total(t, cols, y_part):
            nc.vector.scalar_tensor_tensor(total[:, t, cols], y_part, 1.7, dual_plane[t][:, cols], ALU.mult, ALU.add)

        for u, skip in enumerate((P, 0)):
            make_t0(0, halves[u], y[u, 0][:])
            make_total(0, slice(u * HALF + skip, (u + 1) * HALF), y[u, 0][:, skip:HALF])
        for u in range(2):
            for t in range(2, PACK):
                make_t0(t, halves[u], y[u, t][:])
        make_t0(1, slice(0, S), y[0, 1][:])
        make_total(1, slice(P, S), y[0, 1][:, P:S])
        w2_grouped = []

        def round_w2(h):
            grouped = sb.tile([P, P, PACK], BF16, name="w2_grouped%d" % h, align_bytes=ROW)
            nc.scalar.copy(
                grouped[:].rearrange("p (c i) j -> p c j i", i=4),
                w2_raw[:, :, h * P : (h + 1) * P].rearrange("p j (c i) -> p c j i", i=4),
            )
            w2_grouped.append(grouped)

        def add_turned(t, src, start=False, stop=False):
            nc.tensor.matmul(
                turned[t // 2][:, t % 2, :], src[:, t, 0:P], identity[:], start=start, stop=stop, is_transpose=True
            )

        def turn_back(a, tag):
            pairs = sb.tile([P, P, 2], BF16, name="pairs%d" % a, tag=tag, align_bytes=ROW)
            nc.scalar.copy(pairs[:], turned[a][:].rearrange("j e p -> j p e"))
            nc.tensor.transpose(back[:, a, :], pairs[:].rearrange("j p e -> j (p e)").bitcast(F32), identity[:])

        w2_scales = sb.tile([P, N], U8, name="w2_scales", align_bytes=ROW)

        def quantize_w2(h):
            nc.vector.quantize_mx(
                out=w2_codes[:, h * P : (h + 1) * P].bitcast(FP8X4),
                scales=w2_scales[:, h * P : (h + 1) * P],
                in_=w2_grouped[h][:].rearrange("p c j -> p (c j)"),
            )

        for h in range(OUT_BLOCKS):
            round_w2(h)
        linear = sb.tile([P, PACK, S], F32, name="linear", tag="w2_raw", align_bytes=ROW)
        dual_term = sb.tile([P, PACK, P], F32, name="dual_term", align_bytes=ROW)
        for t in (0, 2, 3, 1):
            nc.scalar.activation(dual_term[:, t, :], dual_plane[t][:, 0:P], COPY, scale=rho_neg[:, t : t + 1])
            if t < 2:
                nc.scalar.activation(linear[:, t, 0:P], y[0, t][:, 0:P], COPY, scale=rho_y[:, t : t + 1])
        for t in range(PACK):
            cols = slice(P if t < 2 else 0, S)
            nc.scalar.activation(linear[:, t, cols], total[:, t, cols], COPY, scale=rho_neg[:, t : t + 1])
        turned = [ps.tile([P, 2, P], F32, name="turned%d" % a, tag="bank%d" % (5 + 2 * a)) for a in range(2)]
        back = ps.tile([P, 2, P], F32, name="back", tag="bank6")
        for t in range(PACK):
            add_turned(t, dual_term, start=t % 2 == 0)
            add_turned(t, linear)

        chunks = [slice(q * P, (q + 1) * P) for q in range(CHUNKS)]
        scaled = sb.tile([P, PACK, S], F32, name="scaled", align_bytes=ROW)

        def scale_clip(t, cols, clip):
            nc.scalar.activation(scaled[:, t, cols], clip, COPY, scale=rho_clip[:, t : t + 1])

        for t in range(2):
            nc.vector.tensor_tensor(t0[:, t, :], t0[:, t, :], low_first[t][:], ALU.max)
        w2_codes = sb.tile([P, N], U32, name="w2_codes", tag="low_first0", align_bytes=ROW)
        for h in range(OUT_BLOCKS):
            quantize_w2(h)
        clip_first = sb.tile([P, 2, S], F32, name="clip_first", align_bytes=ROW)
        for t in range(2):
            nc.vector.tensor_tensor(clip_first[:, t, :], t0[:, t, :], high_first[:, t, :], ALU.min)
            scale_clip(t, slice(0, S), clip_first[:, t, :])
            add_turned(t, scaled, stop=t == 1)
        for n, cols in enumerate(chunks):
            part = slice(n % 2 * P, (n % 2 + 1) * P)
            if n % 2 == 0:
                for m in range(2):
                    both = chunks[n + m]
                    nc.vector.tensor_tensor(
                        t0[:, 2:PACK, both], t0[:, 2:PACK, both], low_second[n // 2][:, :, m * P : (m + 1) * P], ALU.max
                    )
            clip = sb.tile([P, 2, P], F32, name="clip%d" % n, tag="clip%d" % n, align_bytes=ROW)
            nc.vector.tensor_tensor(clip[:], t0[:, 2:PACK, cols], high_second[n // 2][:, :, part], ALU.min)
            for e in range(2):
                scale_clip(2 + e, cols, clip[:, e, :])
                if n == 0:
                    add_turned(2 + e, scaled, stop=e == 1)
            if n % 2 == 0:
                turn_back(n // 2, "clip%d" % n)
        rr_first = sb.tile([P, P, PACK], BF16, name="rr0", align_bytes=ROW)
        nc.scalar.copy(
            rr_first[:].rearrange("p j t -> p (j t)").bitcast(F32).rearrange("p (j a) -> p j a", a=2),
            back[:].rearrange("p a j -> p j a"),
        )

        out_blocks = out.rearrange("(h p) j -> p h j", p=P)
        rr, codes, scales, acc = {0: rr_first}, {}, {}, {}

        def residual(q):
            rr[q] = sb.tile([P, P, PACK], BF16, name="rr%d" % q, align_bytes=ROW)
            nc.vector.tensor_tensor(
                rr[q][:].rearrange("p (c i) t -> p c t i", i=2),
                scaled[:, :, chunks[q]].rearrange("p t (c i) -> p c t i", i=2),
                linear[:, :, chunks[q]].rearrange("p t (c i) -> p c t i", i=2),
                ALU.add,
            )

        def quantize(q):
            codes[q] = sb.tile([P, P], U32, name="rr_codes%d" % q, align_bytes=ROW)
            scales[q] = sb.tile([P, P], U8, name="rr_scales%d" % q, align_bytes=ROW)
            nc.vector.quantize_mx(
                out=codes[q][:].bitcast(FP8X4), scales=scales[q][:], in_=rr[q][:].rearrange("p j t -> p (j t)")
            )

        def product(q):
            acc[q] = ps.tile([P, OUT_BLOCKS, P], F32, name="acc%d" % q, tag="bank%d" % q)
            for h in range(OUT_BLOCKS):
                nc.tensor.matmul_mx(
                    out=acc[q][:, h, :],
                    lhsT=w2_codes[:, h * P : (h + 1) * P].bitcast(FP8X4),
                    lhsT_scale=w2_scales[:, h * P : (h + 1) * P],
                    rhs=codes[q][:].bitcast(FP8X4),
                    rhs_scale=scales[q][:],
                    start=True,
                    stop=True,
                )

        def finish(q):
            res = sb.tile([P, OUT_BLOCKS, P], F32, name="res%d" % q, align_bytes=ROW)
            nc.vector.tensor_tensor(res[:], acc[q][:], lin_sb[:, :, chunks[q]], ALU.add)
            nc.sync.dma_start(out=out_blocks[:, :, chunks[q]], in_=res[:])

        residual(1)
        residual(2)
        for q in (1, 2):
            quantize(q)
            product(q)
        residual(3)
        for q in (0, 3):
            quantize(q)
            product(q)
        for q in (1, 2, 0):
            finish(q)
        last = CHUNKS - 1
        for h in range(OUT_BLOCKS):
            res = sb.tile([P, P], F32, name="res_last%d" % h, align_bytes=ROW)
            nc.vector.tensor_tensor(res[:], acc[last][:, h, :], lin_sb[:, h, chunks[last]], ALU.add)
            nc.sync.dma_start(out=out_blocks[:, h, chunks[last]], in_=res[:])
